import numpy as np, ml_dtypes
CORES = [2,6,10,14,18,22,26,30]
N = 8
import mx_ref
BF = ml_dtypes.bfloat16
def cols(t, e):
    v = np.concatenate([t.reshape(128, -1, 4), np.zeros((128, 1, 4), BF)], axis=1)
    return np.ascontiguousarray(v[:, e]).reshape(128, -1)
def cut(t, i, w=512):
    return t[:, w * i:w * i + w]
def pick(q, e):
    c = np.concatenate([q[0].reshape(128, -1, 4), np.zeros((128, 1, 4), np.uint8)], axis=1); s = np.concatenate([q[1], np.ones((16, 1), np.uint8)], axis=1)
    return (np.ascontiguousarray(c[:, e].reshape(128, -1)), np.ascontiguousarray(s[:, e]))
def join(*qs):
    return (np.concatenate([q[0] for q in qs], axis=1), np.concatenate([q[1] for q in qs], axis=1))
def put(q, e, v):
    c, s = q[0].reshape(128, -1, 4).copy(), q[1].copy(); c[:, e] = v[0].reshape(128, -1, 4); s[:, e] = v[1]
    return (c.reshape(128, -1), s)
def pk(c, s):
    return (np.ascontiguousarray(c), mx_ref.live(s))
def emit(q):
    return q[0], q[1]
def decode(q):
    o = []
    for b in range(4):
        e = np.zeros((128, 128, 4), np.float32); e[np.arange(128), np.arange(128), b] = 1
        o.append(mx_ref.matmul(mx_ref.quantize(e.reshape(128, 512).astype(BF)), q))
    return np.stack(o, axis=2).reshape(128, -1)
def f(rng, *shape):
    return mx_ref.flush((rng.standard_normal(shape, dtype=np.float32) * np.exp2(rng.integers(-2, 3, shape[:-1] + (1,)))).astype(BF))
def wide(rng, *shape, cols=0):
    v = rng.standard_normal(shape, dtype=np.float32) * np.exp2(rng.integers(-12, 13, shape)).astype(np.float32)
    if cols: v *= np.repeat(np.exp2(rng.integers(-cols, cols + 1, shape[:-2] + (1, shape[-1] // 4))) * (rng.random(shape[:-2] + (1, shape[-1] // 4)) > 0.0625), 4, axis=-1).astype(np.float32)
    return mx_ref.flush(v.astype(BF))
M, A, E, R, O = 256, 16, 32, 2, 1
def big(v):
    v = v.astype(np.float32)
    v[np.abs(v) < np.float32(2.0 ** -14)] = 0
    return v.astype(BF)
def plain(rng):
    return {"me": big(f(rng, N, 128, 4 * M)), "x": big(f(rng, N, 128, 4 * A)), "w": f(rng, N, 128, 512 * O)}
def signs(rng, n):
    h = np.ones((1, 1))
    while len(h) < n: h = np.block([[h, h], [h, -h]])
    return h[rng.permutation(n)[:128]][:, rng.permutation(n)] * rng.choice([-1.0, 1.0], n)
def tiles(v):
    return v.reshape(-1, 128, 4).transpose(1, 0, 2).reshape(128, -1)
def store(rng, m, q):
    return {"me": big(np.stack([tiles(v) for v in m.reshape(N, M, 512)])), "x": big(np.stack([tiles(v) for v in q.reshape(N, A, 512)])), "w": f(rng, N, 128, 512 * O)}
def low(rng):
    return rng.standard_normal((N * M, 512), dtype=np.float32) * np.float32(2.0 ** -6)
def rough(rng, v):
    return v * (1 + 0.0625 * rng.uniform(-1, 1, v.shape)) * np.exp2(rng.integers(0, 2, (len(v), 1)))
def places(rng, s):
    at = np.zeros(len(s), int)
    for r in range(N):
        j = np.flatnonzero(s == r)
        at[j] = r * M + rng.permutation(M)[:len(j)]
    return at
def spare(rng, r, at):
    return rng.permutation(np.setdiff1d(np.arange(r * M, r * M + M), at))
def planted(rng, at, o):
    k, i = np.unique(at, return_inverse=True)
    v, m = signs(rng, 512), low(rng)
    m[k] = rough(rng, v[:len(k)])
    m[at[o[0]]] *= 8
    q = rough(rng, v[i])
    q[o[0]] = 4 * v[i[o[0]]] + 8 * v[i[o[-1]]]
    q[o[2]] = q[o[1]]
    return store(rng, m, q)
def setup_inputs(rng):
    return plain(rng)
def setup_inputs_hot(rng):
    h = int(rng.integers(0, N))
    g = (h + int(rng.integers(1, N))) % N
    at = (h + rng.integers(1, N, 128)) % N * M + rng.integers(0, M, 128)
    o = np.flatnonzero(np.arange(128) // A != h)
    p, u = h * M + rng.permutation(M)[:7], g * M + rng.permutation(M)[:6]
    at[o] = u[rng.integers(0, 6, len(o))]
    k = np.concatenate([o[:A], rng.permutation(o[A:-1])[:len(o) // 2 - A - 1]])
    at[k] = p[rng.integers(0, 6, len(k))]
    at[o[2]] = at[o[1]]
    at[o[-1]] = p[6]
    return planted(rng, at, o)
def setup_inputs_ties(rng):
    d, b = plain(rng), int(rng.integers(2, N))
    g = np.full((N, 4), 4.0)
    g[b] = 1
    g[(b + int(rng.integers(1, N))) % N] = 16
    p = big(np.abs(f(rng, 128, 16 * N).astype(np.float32)) * np.repeat(g.reshape(-1), 4))
    k = f(rng, 128, 120).astype(np.float32)
    k[:, :96] = np.abs(k[:, :96])
    k[:, :48] = -k[:, :48]
    k[:, :16] = k[:, :16] * np.float32(2.0 ** 24)
    k = big(k)
    e = rng.permutation(np.concatenate([np.arange(30), rng.integers(12, 24, 58), rng.integers(0, 30, 40)]))
    m = []
    for r in range(N):
        own = np.concatenate([4 * r + np.arange(4), 4 * ((r + 1) % N) + np.arange(4)])
        m.append(cols(p, rng.permutation(np.concatenate([own, own, own[rng.integers(0, 8, M - 16)]]))))
    d["me"] = np.stack(m)
    d["x"] = np.stack([cols(k, e[r * A:r * A + A]) for r in range(N)])
    return d
def setup_inputs_second(rng):
    a, b = signs(rng, 256), signs(rng, 256)
    s = rng.permutation(np.arange(128) % N)
    p = places(rng, np.concatenate([s, (s + rng.integers(1, N, 128)) % N]))
    e = rng.permutation(512)
    e, g = e[:256], e[256:]
    m, q = low(rng), rng.uniform(-1, 1, (128, 512)) * 2.0 ** -6
    q[:, e] = a
    m[p[:128, None], e] = a
    m[p[:128, None], g] = 4 * b
    m[p[128:, None], g] = 16 * b
    return store(rng, m, q)
def setup_inputs_idle(rng):
    o = rng.permutation(N)
    s = o[rng.integers(2, N, 128)]
    s[rng.permutation(128)[:E]] = o[1]
    at = places(rng, s)
    j = int(np.argmin(s))
    z = np.sort(spare(rng, int(s[j]), at)[:2])
    at[j] = z[0]
    far = spare(rng, int(s.max()), at)[0]
    v, m = signs(rng, 512), low(rng)
    v = v * v[j]
    m[at] = rough(rng, v)
    m = m - np.float32(0.25)
    m[[z[0], z[1], far]] = 0
    q = rough(rng, v)
    q[j] = 2 * q[j]
    d = store(rng, m * np.float32(2.0 ** 27), q * 2.0 ** 27)
    c = 4 * int(z[0] % M)
    d["me"][int(s[j]), :, c:c + 4] = BF(-0.0)
    return d
def setup_inputs_spread(rng):
    return {**plain(rng), "me": big(wide(rng, N, 128, 4 * M, cols=3)), "x": big(wide(rng, N, 128, 4 * A, cols=3))}
def check_inputs(d):
    b = []
    for k, least in (("me", 2.0 ** -14), ("x", 2.0 ** -14), ("w", 2.0 ** -30)):
        v = np.abs(d[k].astype(np.float32))
        if not (np.isfinite(v).all() and ((v == 0) | (v >= least) & (v <= 2.0 ** 30)).all()): b.append("a value of " + k)
    return b
def reference(me, x, w):
    mem = [mx_ref.quantize(np.ascontiguousarray(me[r])) for r in range(N)]
    q = join(*[mx_ref.quantize(np.ascontiguousarray(x[r])) for r in range(N)])
    wi = np.zeros((N, R, 128), np.float32)
    for t in range(R):
        s = np.concatenate([mx_ref.matmul(q, mem[r]) for r in range(N)], axis=1) + np.float32(0)
        win = np.argmax(s, axis=1)
        answered = np.zeros(128, bool)
        for r in range(N): answered[np.flatnonzero(win // M == r)[:E]] = True
        wi[:, t] = np.where(answered, win, -1 - win)
        half = decode(pick(join(*mem), win)) * np.float32(0.5)
        new = mx_ref.quantize((half + decode(q) * np.float32(0.5)).astype(BF))
        a = np.flatnonzero(answered)
        q = put(q, a, pick(new, a))
        for r in range(N):
            j = a[win[a] // M == r]
            if j.size:
                c, i = np.unique(win[j] - r * M, return_index=True)
                mem[r] = put(mem[r], c, pick(new, j[i]))
    oc, osc, y = np.zeros((N, 128, 4 * M), np.uint8), np.zeros((N, 16, M), np.uint8), np.zeros((N, 128, 128 * O), np.float32)
    for r in range(N):
        oc[r], osc[r] = emit(mem[r])
        for o in range(O): y[r, :, 128 * o:128 * o + 128] = mx_ref.matmul(mx_ref.quantize(np.ascontiguousarray(cut(w[r], o))), q)
    return {"oc": oc, "osc": osc, "wi": wi, "y": y}

@@ -1,0 +1,424 @@
+from concourse.bass import DstId, RemoteDMATransfer
+from concourse.mybir import dt, AluOpType, AxisListType, ActivationFunctionType
+
+N, M, A, E, R = 8, 256, 16, 32, 2
+NQ = N * A
+OP = AluOpType
+AF = ActivationFunctionType
+AX = AxisListType.X
+BIG = 1.0e9
+LOW = -9.0e29
+OUT = 65536.0
+
+WORK = [("ti", 8), ("sl", 16), ("ra", 32), ("ru", 32), ("fr", 32), ("oh", 32), ("cb", 32), ("rc", 32), ("la", 128),
+        ("ly", 128), ("ft", 128), ("cn", 128), ("sa", 128), ("sb", 128), ("acc", 8), ("ot", 128), ("ct", 128), ("lc", 128),
+        ("oy", 128), ("rl", 8), ("tw", 8), ("t1", 8), ("kr", 8), ("kk", 8), ("an", 8), ("tt", 8), ("m1", 8), ("m2", 8),
+        ("m3", 8), ("m4", 8), ("ol", 8), ("ix", 8), ("gg", 8), ("b1", 8), ("b2", 8), ("sg", 256), ("ab", 256), ("am", 256)]
+AT = {}
+_n = 0
+for _name, _w in WORK:
+    AT[_name] = (_n, _w)
+    _n += _w
+
+SCRATCH = {
+    "xt": ("sbuf", [128, 512], "bfloat16"), "met": ("sbuf", [128, 4 * M], "bfloat16"),
+    "wt": ("sbuf", [128, 512], "bfloat16"), "et": ("sbuf", [128, 2048], "bfloat16"),
+    "half": ("sbuf", [128, 128], "bfloat16"), "diag": ("sbuf", [128, 128], "bfloat16"),
+    "xq": ("sbuf", [128, 128], "float8_e4m3fn_x4"), "xs": ("sbuf", [128, 128], "uint8"),
+    "wq": ("sbuf", [128, 128], "float8_e4m3fn_x4"), "wz": ("sbuf", [128, 128], "uint8"),
+    "eq": ("sbuf", [128, 512], "float8_e4m3fn_x4"), "ez": ("sbuf", [128, 512], "uint8"),
+    "zz": ("sbuf", [128, 256], "float32"), "wm": ("sbuf", [128, 32], "float32"), "nwm": ("sbuf", [128, 128], "float32"),
+    "wp": ("sbuf", [128, 32], "float32"),
+    "rst": ("sbuf", [128, 256], "float32"), "lp": ("sbuf", [128, 128], "int32"), "la": ("sbuf", [128, 128], "int32"),
+    "ip": ("sbuf", [128, 8], "int32"), "ia": ("sbuf", [128, 8], "int32"), "kf": ("sbuf", [128, 32], "float32"),
+    "kq": ("sbuf", [128, 32], "float32"), "c16": ("sbuf", [128, 16], "float32"), "cp": ("sbuf", [128, 16], "float32"),
+    "cc": ("sbuf", [128, 8], "float32"), "cn": ("sbuf", [128, 8], "float32"),
+    "cst": ("sbuf", [128, 32], "float32"), "yt": ("sbuf", [128, 128], "float32"),
+    "idl": ("sbuf", [128, 16], "uint16"), "lidx": ("sbuf", [128, 32], "float32"),
+    "psc": ("psum", [128, 512], "float32"), "pbl": ("psum", [128, 2048], "float32"), "pyy": ("psum", [128, 512], "float32"),
+}
+for _t in range(R + 1):
+    SCRATCH["mq%d" % _t] = ("sbuf", [128, M], "float8_e4m3fn_x4")
+    SCRATCH["mz%d" % _t] = ("sbuf", [128, M], "uint8")
+    SCRATCH["qa%d" % _t] = ("sbuf", [128, NQ], "float8_e4m3fn_x4")
+    SCRATCH["qz%d" % _t] = ("sbuf", [128, NQ], "uint8")
+for _t in range(R):
+    for _name, _w, _d in (("mw", M + E, "float8_e4m3fn_x4"), ("mx", M + E, "uint8"),
+                          ("win", NQ + N * E, "float8_e4m3fn_x4"), ("wis", NQ + N * E, "uint8"),
+                          ("pm", NQ, "float8_e4m3fn_x4"), ("pz", NQ, "uint8"),
+                          ("nq", 160, "float8_e4m3fn_x4"), ("nz", 160, "uint8"),
+                          ("nt", 520, "bfloat16"), ("run", 264, "float32"), ("land", 32, "float32"),
+                          ("ri", 136, "float32"), ("uu", 32, "float32"), ("wv", 8, "float32"), ("f", _n, "float32"),
+                          ("offi", 8, "uint16"), ("offs", 2, "uint16"), ("offm", 16, "uint16"), ("offq", 8, "uint16")):
+        SCRATCH["%s%d" % (_name, _t)] = ("sbuf", [128, _w], _d)
+
+ONCE = ["ldx", "ldm", "ldw", "ixt", "ihf", "gdi", "gip", "xqd", "eqd", "wqd", "qx", "oq", "mq0", "vcc", "vco", "vid",
+        "ls", "idx", "oli", "orn", "yp", "yc", "st", "sty"]
+EACH = ["sc", "rn", "ix", "ow", "oi", "pm", "ba", "bb", "bc", "bd", "nt", "nq", "ar", "ac", "os", "sl", "u1", "ab",
+        "om", "mp", "od", "nx", "on", "qp", "mc", "qc", "wi", "va", "vu", "vb", "vk", "vc", "vm", "vw"]
+SEMAPHORES = ONCE + ["%s%d" % (_s, _t) for _s in EACH for _t in range(R)]
+QUARTERS = (0, 32, 64, 96)
+
+
+def rank_program(g, core, T, topo):
+    rank = T.rank_of(core)
+    if rank is None:
+        return
+    V, S, P, Y = g.vector, g.scalar, g.tensor, g.sync
+    queue = {"v": V, "s": S, "t": P, "y": Y, "g": g}
+    total, seen = {}, {}
+
+    def up(ins, name, n=1):
+        ins.then_inc(T.sem[name], n)
+        total[name] = total.get(name, 0) + n
+
+    def wait(q, *names):
+        for name in names:
+            if seen.get((q, name), 0) < total[name]:
+                queue[q].wait_ge(T.sem[name], total[name])
+                seen[(q, name)] = total[name]
+                seen[("", name)] = total[name]
+
+    def u32(name, a, b):
+        return T[name][:, a:b].bitcast(dt.uint32)
+
+    def u8(name, a, b):
+        return T[name][:, a:b].bitcast(dt.uint8)
+
+    here = topo.chip(core)
+
+    def near(c):
+        k = topo.chip(c)
+        return (2 if topo.mates(here, k) else 1 if topo.same_plane(here, k) else 0, topo.die(c) != topo.die(core))
+
+    off = sorted([c for c in T.cores if topo.chip(c) != here], key=near)
+    on = [c for c in T.cores if c != core and topo.chip(c) == here]
+    common = topo.mask(core, off[0])
+    for c in off:
+        common = common & topo.mask(core, c)
+    free = [e for e in topo.engines(core, on[0]) if not common >> e & 1]
+    local = (1 << free[0]) | (1 << free[len(free) // 2])
+    n_off = sum(common >> e & 1 for e in range(common.bit_length()))
+    arrive = len(off) * n_off + len(on) * 2
+
+    def dst(c):
+        rid, pid = topo.addr(c)[:2]
+        return DstId(rid=rid, pnc=pid)
+
+    def send(src, out, sem):
+        g.remote_dma_fused([
+            RemoteDMATransfer(dst_ids=[dst(c) for c in off], dma_engine_mask=common, remote_sem=T.sem[sem],
+                              srcs=[src], dsts=[out for c in off]),
+            RemoteDMATransfer(dst_ids=[dst(c) for c in on], dma_engine_mask=local, remote_sem=T.sem[sem],
+                              srcs=[src], dsts=[out for c in on])], local_sem=T.sem["ls"])
+        total["ls"] = total.get("ls", 0) + n_off + 2
+        total[sem] = total.get(sem, 0) + arrive
+
+    up(Y.dma_start(T.xt[:, 0:4 * A], T.x[:]), "ldx", 16)
+    up(Y.dma_start(T.met[:], T.me[:]), "ldm", 16)
+    up(Y.dma_start(T.wt[:], T.w[:]), "ldw", 16)
+
+    up(V.memset(T.xt[:, 4 * A:512], 0.0), "ixt")
+    up(V.memset(T.half[:], 0.5), "ihf")
+    up(V.memset(T.et[:], 0.0), "vcc")
+    up(g.iota(T.ip[:, 0:1], [[1, 1]], 0, 1), "gip")
+    up(g.iota(T.c16[:], [[16, 16]], 0, 0, allow_small_or_imprecise_dtypes=True), "gip")
+    up(g.iota(T.lp[:], [[1, 128]], 128, -1), "gip")
+    up(g.iota(T.kf[:], [[1, 32]], 0, 0, allow_small_or_imprecise_dtypes=True), "gip")
+    wait("g", "ihf")
+    up(g.affine_select(T.diag[:], T.half[:], [[-1, 128]], OP.is_equal, 0.0, 0, 1), "gdi")
+    wait("v", "ldx", "ixt")
+    up(V.quantize_mx(T.xq[:], T.xs[:], T.xt[:]), "xqd")
+    a = A * rank
+    wait("g", "xqd")
+    send(u8("xq", 0, A), u8("qa0", a, a + A), "qx")
+    send(T.xs[:, 0:A], T.qz0[:, a:a + A], "qx")
+    wait("g", "gip", "gdi")
+
+    wait("v", "gip")
+    up(V.tensor_scalar(T.ia[:, 0:1], T.ip[:, 0:1], 15, None, OP.bitwise_and), "vid")
+    up(V.tensor_copy(T.cst[:, 0:1], T.ip[:, 0:1]), "vco")
+    up(V.tensor_scalar(T.la[:], T.lp[:], 15, None, OP.bitwise_and), "vco")
+    wait("v", "vid")
+    up(V.tensor_copy(T.cst[:, 1:2], T.ia[:, 0:1]), "vid")
+    wait("v", "vid")
+    up(V.tensor_scalar(T.cp[:], T.c16[:], T.cst[:, 1:2], None, OP.add), "vid")
+    wait("v", "vid")
+    up(V.tensor_copy(T.idl[:], T.cp[:]), "vid")
+    wait("v", "vid", "xqd")
+    up(V.tensor_copy(u32("qa0", a, a + A), u32("xq", 0, NQ).indirect(T.idl[:, 0:1])), "oq")
+    wait("s", "vid", "xqd")
+    up(S.activation(T.qz0[:, a:a + A], T.xs[:, 0:NQ].indirect(T.idl[:, 0:1]), AF.Copy), "oq")
+    wait("v", "vcc", "gdi")
+    for b in range(4):
+        up(V.tensor_copy(T.et[:, 512 * b + b:512 * b + 512:4], T.diag[:]), "vcc")
+    up(V.memset(T.zz[:], 0.0), "vco")
+    wait("v", "vcc")
+    up(V.quantize_mx(T.eq[:], T.ez[:], T.et[:]), "eqd")
+    wait("v", "ldm")
+    up(V.quantize_mx(T.mq0[:], T.mz0[:], T.met[:]), "mq0")
+    up(V.memset(T.rst[:], -BIG), "vco")
+    for t in range(R):
+        o = AT["oh"][0]
+        up(V.memset(T["f%d" % t][:, o:o + 32], 0.0), "vco")
+        o = AT["sl"][0]
+        up(V.memset(T["f%d" % t][:, o:o + 1], 1.0), "vco")
+        up(V.memset(T["ri%d" % t][:], 1000.0), "vco")
+        up(V.memset(T["nt%d" % t][:, 512:520], 0.0), "vco")
+    up(V.tensor_scalar(T.kq[:], T.kf[:], 1.0 / 64, None, OP.mult), "vco")
+    up(V.tensor_copy(T.cc[0:32, :], T.cp[0:32, 0:8]), "vco")
+    up(V.tensor_copy(T.cc[32:64, :], T.cp[32:64, 8:16]), "vco")
+    wait("v", "mq0")
+    up(V.tensor_copy(u32("mw0", 0, M), u32("mq0", 0, M).indirect(T.idl[:])), "mc0")
+    wait("s", "mq0")
+    up(S.activation(T.mx0[:, 0:M], T.mz0[:].indirect(T.idl[:]), AF.Copy), "mc0")
+    wait("v", "vco")
+    up(V.memset(T.rst[:, 0:256:32], BIG), "vco")
+    up(V.tensor_scalar(T.wm[:], T.la[:, 0:32], 0, None, OP.is_equal), "vco")
+    up(V.tensor_scalar(T.nwm[:], T.la[:], 0, None, OP.not_equal), "vco")
+    up(V.tensor_scalar(T.cst[:, 2:3], T.cst[:, 0:1], -1.0, float(NQ - 1), OP.mult, OP.add), "vco")
+    up(V.tensor_scalar(T.cst[:, 3:4], T.cst[:, 0:1], OUT, None, OP.add), "vco")
+    up(V.tensor_scalar(T.cst[:, 4:5], T.cst[:, 1:2], 0.5, None, OP.add), "vco")
+    up(V.tensor_scalar(T.cst[:, 5:6], T.cst[:, 1:2], 16.5, None, OP.add), "vco")
+    up(V.tensor_scalar(T.cn[0:64, :], T.cc[0:64, :], -1.0, None, OP.mult), "vco")
+    wait("v", "vco")
+    up(V.tensor_scalar(T.wp[:], T.wm[:], T.cst[:, 3:4], -OUT, OP.mult, OP.add), "vco")
+    wait("v", "ldw")
+    up(V.quantize_mx(T.wq[:], T.wz[:], T.wt[:]), "wqd")
+    wait("v", "vco")
+    wait("s", "vco")
+
+    for t in range(R):
+        def B(name, u=t):
+            return T["%s%d" % (name, u)]
+
+        def s(name, u=t):
+            return "%s%d" % (name, u)
+
+        def f(name, a=0, b=None, step=1, u=t):
+            o, w = AT[name]
+            return T["f%d" % u][:, o + a:o + (w if b is None else b):step]
+
+        def h(name, a=0, b=None, step=1, p=0, n=32):
+            o, w = AT[name]
+            return B("f")[p:p + n, o + a:o + (w if b is None else b):step]
+
+        def fold(row, block, sem):
+            for p in QUARTERS:
+                up(V.transpose(row[0:32, p:p + 32], h(block, p=p)), sem)
+
+        def lanes(out, y, sem):
+            for p in QUARTERS:
+                up(V.tensor_copy(out[p:p + 32, 0:8], h(y, 15, 128, 16)), sem)
+
+        def number(step, u=t):
+            where = T.land1[:, 1:32:4] if u == 0 else T.lidx[:, 0:32:4]
+            one, vw = (0, 1, 1, u), s("vw", u)
+            wait("v", vw)
+            if step == 0:
+                up(V.tensor_tensor(f("ol", 0, 8, 1, u), f("oh", 0, 8, 1, u), where, OP.mult), vw)
+            elif step == 1:
+                up(V.tensor_reduce(f("ix", *one), f("ol", 0, 8, 1, u), AX, OP.add), vw)
+            elif step == 2:
+                up(V.tensor_scalar(f("gg", *one), f("tw", *one), float(M), f("ix", *one), OP.mult, OP.add), vw)
+            else:
+                up(V.tensor_scalar(B("wv", u)[:, 0:1], f("gg", *one), f("b2", *one), f("b1", *one), OP.mult, OP.add),
+                   s("wi", u))
+
+        one = (0, 1)
+        va, vu, vb, vk, vc, vm = s("va"), s("vu"), s("vb"), s("vk"), s("vc"), s("vm")
+        mq, mz, qa, qz = B("mq"), B("mz"), B("qa"), B("qz")
+        if t == 0:
+            wait("t", "mq0", "oq", "qx")
+        else:
+            wait("t", s("mp", 0), s("rn", 0), s("qp", 0))
+        up(P.matmul_mx(T.psc[:, 0:M], qa[:], qz[:], mq[:], mz[:], True, True), s("sc"))
+        wait("t", "eqd")
+        if t:
+            wait("t", s("nt", 0))
+        for b in (0, 2, 1, 3):
+            P.matmul_mx(T.pbl[:, 512 * b:512 * b + NQ], T.eq[:, 128 * b:128 * b + 128], T.ez[:, 128 * b:128 * b + 128],
+                        qa[:], qz[:], True, False)
+        run, land, k = B("run"), B("land"), 4 * rank
+        wait("v", s("sc"))
+        up(V.tensor_tensor_scan(run[:, 0:M], T.psc[:, 0:M], T.zz[:], LOW, OP.max, OP.add), s("rn"))
+        wait("g", s("rn"))
+        if t == 0:
+            send(run[:, M - 1:M], land[:, k:k + 1], s("ar"))
+        else:
+            wait("g", "orn")
+            send(run[:, M - 1:M + 1], land[:, k:k + 2], s("ar"))
+        wait("s", s("rn"))
+        up(S.activation(f("sg"), run[:, 0:M], AF.Sign, bias=run[:, M - 1:M], scale=-1.0, accum_out=f("ti", *one)), s("ix"))
+        up(S.activation(land[:, k:k + 1], run[:, M - 1:M], AF.Copy), s("ow"))
+        if t == 0:
+            wait("v", "oq", "qx")
+            wait("s", "oq", "qx")
+            up(V.tensor_copy(u32("win0", 0, NQ), u32("qa0", 0, NQ).indirect(T.idl[:, 0:8])), s("qc"))
+            up(S.activation(T.wis0[:, 0:NQ], T.qz0[:, 0:NQ].indirect(T.idl[:, 0:8]), AF.Copy), s("qc"))
+        else:
+            up(V.tensor_copy(u32("win1", 0, NQ), u32("win0", 0, NQ + N * E).indirect(T.offq0[:, 0:8])), s("qc"))
+            up(S.activation(T.wis1[:, 0:NQ], T.wis0[:, 0:NQ + N * E].indirect(T.offq0[:, 0:8]), AF.Copy), s("qc"))
+            wait("g", s("ix"))
+            send(f("ti", *one), T.lidx[:, k:k + 1], "idx")
+            wait("y", s("mp", 0), s("ar"))
+            up(Y.dma_start(u8("mw1", 0, M), u8("mq1", 0, M)), "mc1", 16)
+            up(Y.dma_start(T.mx1[:, 0:M], T.mz1[:]), "mc1", 16)
+        wait("v", s("ix"))
+        up(V.tensor_scalar(f("ra"), T.wm[:], f("ti", *one), None, OP.mult), va)
+        up(V.tensor_scalar(f("ru"), T.zz[:, 0:32], f("ti", *one), None, OP.add), vu)
+        wait("v", va)
+        fold(f("la"), "ra", va)
+        wait("v", va)
+        up(V.tensor_tensor_scan(h("ly"), T.nwm[0:32, :], h("la"), 0.0, OP.mult, OP.add), va)
+        wait("v", va)
+        lanes(B("offi"), "ly", s("oi"))
+        wait("v", s("oi"))
+        up(V.tensor_copy(u32(s("pm"), 0, NQ), u32(s("mq"), 0, M).indirect(B("offi")[:, 0:8])), s("pm"))
+        wait("s", s("oi"))
+        up(S.activation(B("pz")[:, 0:NQ], mz[:, 0:M].indirect(B("offi")[:, 0:8]), AF.Copy), s("pm"))
+        ri = B("ri")
+        wait("v", vu)
+        fold(ri, "ru", vu)
+        wait("t", s("pm"))
+        bank = {0: s("ba"), 1: s("bb"), 2: s("bc"), 3: s("bd")}
+        for b in (0, 2, 1, 3):
+            up(P.matmul_mx(T.pbl[:, 512 * b:512 * b + NQ], T.eq[:, 128 * b:128 * b + 128], T.ez[:, 128 * b:128 * b + 128],
+                           B("pm")[:], B("pz")[:], False, True), bank[b])
+        nt = B("nt")
+        for b in (0, 1):
+            wait("v", bank[b])
+            up(V.tensor_copy(nt[:, b:512:4], T.pbl[:, 512 * b:512 * b + NQ]), s("nt"))
+        for b in (2, 3):
+            wait("s", bank[b])
+            up(S.activation(nt[:, b:512:4], T.pbl[:, 512 * b:512 * b + NQ], AF.Copy), s("nt"))
+        wait("v", s("nt"))
+        up(V.quantize_mx(B("nq")[:, 0:130], B("nz")[:, 0:130], nt[:]), s("nq"))
+        wait("v", vu)
+        up(V.tensor_copy(ri[32:64, 0:NQ], ri[0:32, 0:NQ]), vu)
+        wait("s", s("ix"))
+        if t == 0:
+            up(S.activation(T.run1[:, M:M + 1], f("ti", *one), AF.Copy), "orn")
+            up(S.activation(T.land1[:, k + 1:k + 2], f("ti", *one), AF.Copy), "orn")
+        else:
+            up(S.activation(T.lidx[:, k:k + 1], f("ti", *one), AF.Copy), "oli")
+        wait("v", s("ow"), s("ar"))
+        up(V.tensor_tensor_scan(f("rl"), land[:, 0:32:4], T.zz[:, 0:8], LOW, OP.max, OP.add), vb)
+        wait("v", vb)
+        up(V.tensor_scalar(f("sl", 1, 9), f("rl"), f("rl", 7, 8), None, OP.is_lt), vb)
+        wait("v", vb)
+        up(V.tensor_scalar(f("fr"), T.zz[:, 0:32], f("sl", rank, rank + 1), f("sl", rank + 1, rank + 2), OP.add,
+                           OP.subtract), vb)
+        up(V.tensor_tensor(f("oh", 0, 8), f("sl", 0, 8), f("sl", 1, 9), OP.subtract), vc)
+        wait("v", vb)
+        fold(f("ft"), "fr", vb)
+        up(V.tensor_reduce(f("tw", *one), f("sl", 1, 9), AX, OP.add), vk)
+        wait("v", vb)
+        up(V.tensor_tensor_scan(h("cn"), h("ft"), T.zz[0:32, 0:128], 0.0, OP.add, OP.add), vb)
+        wait("s", vb)
+        up(S.activation(h("sa"), h("cn"), AF.Sign, bias=T.cst[0:32, 4:5], scale=-1.0, accum_out=h("acc", 0, 1)), s("ac"))
+        up(S.activation(h("sb"), h("cn"), AF.Sign, bias=T.cst[0:32, 5:6], scale=-1.0, accum_out=h("acc", 1, 2)), s("ac"))
+        wait("v", vc)
+        fold(f("ot"), "oh", vc)
+        wait("v", vc)
+        up(V.tensor_tensor_scan(h("ct"), h("ot"), T.zz[0:32, 0:128], 0.0, OP.add, OP.add), vc)
+        wait("v", s("ac"), s("nq"))
+        offs = B("offs")
+        for p in QUARTERS:
+            up(V.tensor_scalar(offs[p:p + 32, 0:2], h("acc", 0, 2), 0.5, 64.0, OP.mult, OP.add), s("os"))
+        wait("v", s("os"))
+        up(V.tensor_copy(u32(s("mw"), M, M + E), u32(s("nq"), 0, 130).indirect(offs[:, 0:2])), s("sl"))
+        wait("s", s("nq"), s("os"))
+        up(S.activation(B("mx")[:, M:M + E], B("nz")[:, 0:130].indirect(offs[:, 0:2]), AF.Copy), s("sl"))
+        wait("g", s("sl"))
+        e = NQ + E * rank
+        send(u8(s("mw"), M, M + E), u8(s("win"), e, e + E), s("nx"))
+        send(B("mx")[:, M:M + E], B("wis")[:, e:e + E], s("nx"))
+        wait("v", vu)
+        up(V.tensor_tensor(B("uu")[:, 0:E], ri[:, 0:136].indirect(offs[:, 0:2]), T.kq[:], OP.add), s("u1"))
+        wait("s", s("u1"))
+        for c in range(8):
+            up(S.activation(h("ab", 32 * c, 32 * c + 32, n=64), B("uu")[0:64, 0:E], AF.Abs, bias=T.cn[0:64, c:c + 1],
+                            scale=1.0), s("ab"))
+        up(S.activation(B("wis")[:, e:e + E], B("nz")[:, 0:130].indirect(offs[:, 0:2]), AF.Copy), s("on"))
+        wait("v", vc)
+        for p in QUARTERS:
+            up(V.transpose(h("cb", p=p), h("ct", p, p + 32)), vc)
+        wait("v", vk)
+        up(V.tensor_scalar(f("t1", *one), f("tw", *one), float(E), T.cst[:, 2:3], OP.mult, OP.add), vk)
+        wait("v", vc)
+        up(V.tensor_tensor(f("kr"), f("cb", 0, 8), f("oh", 0, 8), OP.mult), vc)
+        up(V.tensor_copy(u32(s("win"), e, e + E), u32(s("nq"), 0, 130).indirect(offs[:, 0:2])), s("on"))
+        wait("v", vc)
+        up(V.tensor_reduce(f("kk", *one), f("kr"), AX, OP.add), vc)
+        if t:
+            wait("v", "orn")
+            number(0, 0)
+        wait("v", vc)
+        up(V.tensor_scalar(f("an", *one), f("kk", *one), E + 0.5, None, OP.is_lt), vc)
+        if t:
+            number(1, 0)
+        wait("v", vc, vk)
+        up(V.tensor_scalar(f("tt", *one), f("kk", *one), f("t1", *one), f("an", *one), OP.add, OP.mult), vc)
+        up(V.tensor_scalar(f("b2", *one), f("an", *one), 2.0, -1.0, OP.mult, OP.add), s("vw"))
+        up(V.tensor_scalar(f("b1", *one), f("an", *one), -1.0, None, OP.add), s("vw"))
+        wait("v", vc)
+        up(V.tensor_scalar(f("rc"), T.wp[:], f("tt", *one), 0.0, OP.add, OP.max), vc)
+        if t:
+            number(2, 0)
+        wait("v", vc)
+        fold(f("lc"), "rc", vc)
+        if t:
+            number(3, 0)
+        wait("v", s("ab"))
+        up(V.tensor_tensor_scan(h("am", n=64), T.rst[0:64, :], h("ab", n=64), 0.0, OP.max, OP.min), vm)
+        wait("v", vc)
+        up(V.tensor_tensor_scan(h("oy"), T.nwm[0:32, :], h("lc"), 0.0, OP.mult, OP.add), vc)
+        wait("v", vm)
+        low = h("am", 31, 256, 32, n=64)
+        up(V.tensor_scalar(h("m1", n=64), low, 0.5, None, OP.is_lt), vm)
+        up(V.tensor_scalar(h("m2", n=64), low, 64.0, float(M), OP.mult, OP.add), vm)
+        if t:
+            wait("v", "idx", "oli")
+            number(0, 1)
+        wait("v", vm)
+        up(V.tensor_tensor(h("m3", n=64), h("m1", n=64), h("m2", n=64), OP.mult), vm)
+        if t:
+            number(1, 1)
+        wait("v", vm)
+        up(V.tensor_tensor(h("m4", n=64), h("m3", n=64), T.cc[0:64, :], OP.max), vm)
+        wait("v", vc)
+        lanes(B("offq"), "oy", s("od"))
+        wait("v", vm)
+        for p in QUARTERS:
+            up(V.tensor_copy(B("offm")[p:p + 32, 0:8], h("m4")), s("om"))
+            up(V.tensor_copy(B("offm")[p:p + 32, 8:16], h("m4", p=32)), s("om"))
+        if t:
+            number(2, 1)
+            number(3, 1)
+        wait("v", s("om"), s("sl"), s("mc"))
+        mp = s("mp")
+        up(V.tensor_copy(u32(s("mq", t + 1), 0, M), u32(s("mw"), 0, M + E).indirect(B("offm")[:, 0:16])), mp)
+        wait("s", s("om"), s("sl"), s("mc"))
+        up(S.activation(B("mz", t + 1)[:, 0:M], B("mx")[:, 0:M + E].indirect(B("offm")[:, 0:16]), AF.Copy), mp)
+        for q in ("v", "s"):
+            wait(q, s("od"), s("on"), s("qc"), s("nx"))
+        up(V.tensor_copy(u32(s("qa", t + 1), 0, NQ), u32(s("win"), 0, NQ + N * E).indirect(B("offq")[:, 0:8])), s("qp"))
+        up(S.activation(B("qz", t + 1)[:, 0:NQ], B("wis")[:, 0:NQ + N * E].indirect(B("offq")[:, 0:8]), AF.Copy), s("qp"))
+
+    wait("y", "wi0", "wi1")
+    for u in range(R):
+        up(Y.dma_start(T.wi[u:u + 1, :], T["wv%d" % u][:, 0:1]), "st", 16)
+    wait("y", "mp1", "nx1")
+    up(Y.dma_start(T.oc[:, 0:4 * M], u8("mq%d" % R, 0, M)), "st", 16)
+    for c in range(4):
+        up(Y.dma_start(T.osc[4 * c:4 * c + 4, 0:M], T["mz%d" % R][32 * c:32 * c + 4, 0:M]), "st", 16)
+    wait("t", "wqd", "qp1")
+    up(P.matmul_mx(T.pyy[:, 0:NQ], T.wq[:], T.wz[:], T.qa2[:], T.qz2[:], True, True), "yp")
+    wait("v", "yp")
+    up(V.tensor_copy(T.yt[:], T.pyy[:, 0:NQ]), "yc")
+    wait("s", "yc")
+    up(S.dma_start(T.y[:], T.yt[:]), "sty", 16)
+    for name in total:
+        if seen.get(("", name), 0) < total[name]:
+            wait("g", name)

@@ -6,19 +6,20 @@ NQ = N * A
 OP = AluOpType
 AF = ActivationFunctionType
 AX = AxisListType.X
-BIG = 1.0e9
 LOW = -9.0e29
 OUT = 65536.0
+FAR = 512.0
 
-WORK = [("ti", 8), ("sl", 16), ("ra", 32), ("ru", 32), ("fr", 32), ("oh", 32), ("cb", 32), ("rc", 32), ("la", 128),
+WORK = [("ti", 8), ("ra", 32), ("ru", 32), ("fr", 32), ("cb", 32), ("rc", 32), ("la", 128), ("rr", 128),
         ("ly", 128), ("ft", 128), ("cn", 128), ("sa", 128), ("sb", 128), ("acc", 8), ("ot", 128), ("ct", 128), ("lc", 128),
-        ("oy", 128), ("rl", 8), ("tw", 8), ("t1", 8), ("kr", 8), ("kk", 8), ("an", 8), ("tt", 8), ("m1", 8), ("m2", 8),
-        ("m3", 8), ("m4", 8), ("ol", 8), ("ix", 8), ("gg", 8), ("b1", 8), ("b2", 8), ("sg", 256), ("ab", 256), ("am", 256)]
+        ("oy", 128), ("rl", 8), ("t0", 8), ("t1", 8), ("kr", 8), ("kk", 8), ("an", 8), ("tt", 8),
+        ("ol", 8), ("ix", 8), ("b2", 8), ("sg", 256), ("ab", 256), ("am", 256)]
 AT = {}
 _n = 0
 for _name, _w in WORK:
     AT[_name] = (_n, _w)
     _n += _w
+RI = NQ + 8
 
 SCRATCH = {
     "xt": ("sbuf", [128, 512], "bfloat16"), "met": ("sbuf", [128, 4 * M], "bfloat16"),
@@ -28,11 +29,12 @@ SCRATCH = {
     "wq": ("sbuf", [128, 128], "float8_e4m3fn_x4"), "wz": ("sbuf", [128, 128], "uint8"),
     "eq": ("sbuf", [128, 512], "float8_e4m3fn_x4"), "ez": ("sbuf", [128, 512], "uint8"),
     "zz": ("sbuf", [128, 256], "float32"), "wm": ("sbuf", [128, 32], "float32"), "nwm": ("sbuf", [128, 128], "float32"),
-    "wp": ("sbuf", [128, 32], "float32"),
-    "rst": ("sbuf", [128, 256], "float32"), "lp": ("sbuf", [128, 128], "int32"), "la": ("sbuf", [128, 128], "int32"),
+    "wp": ("sbuf", [128, 32], "float32"), "tab": ("sbuf", [128, 8], "float32"),
+    "rst": ("sbuf", [128, 256], "float32"), "im": ("sbuf", [128, 128], "float32"),
     "ip": ("sbuf", [128, 8], "int32"), "ia": ("sbuf", [128, 8], "int32"), "kf": ("sbuf", [128, 32], "float32"),
-    "kq": ("sbuf", [128, 32], "float32"), "c16": ("sbuf", [128, 16], "float32"), "cp": ("sbuf", [128, 16], "float32"),
-    "cc": ("sbuf", [128, 8], "float32"), "cn": ("sbuf", [128, 8], "float32"),
+    "c16": ("sbuf", [128, 16], "float32"), "cp": ("sbuf", [128, 16], "float32"),
+    "cn": ("sbuf", [128, 8], "float32"), "ohb": ("sbuf", [128, 32 * R], "float32"),
+    "slb": ("sbuf", [128, 16 * R], "float32"),
     "cst": ("sbuf", [128, 32], "float32"), "yt": ("sbuf", [128, 128], "float32"),
     "idl": ("sbuf", [128, 16], "uint16"), "lidx": ("sbuf", [128, 32], "float32"),
     "psc": ("psum", [128, 512], "float32"), "pbl": ("psum", [128, 2048], "float32"), "pyy": ("psum", [128, 512], "float32"),
@@ -48,16 +50,18 @@ for _t in range(R):
                           ("pm", NQ, "float8_e4m3fn_x4"), ("pz", NQ, "uint8"),
                           ("nq", 160, "float8_e4m3fn_x4"), ("nz", 160, "uint8"),
                           ("nt", 520, "bfloat16"), ("run", 264, "float32"), ("land", 32, "float32"),
-                          ("ri", 136, "float32"), ("uu", 32, "float32"), ("wv", 8, "float32"), ("f", _n, "float32"),
+                          ("ri", RI, "float32"), ("uu", 32, "float32"), ("wv", 8, "float32"), ("f", _n, "float32"),
                           ("offi", 8, "uint16"), ("offs", 2, "uint16"), ("offm", 16, "uint16"), ("offq", 8, "uint16")):
         SCRATCH["%s%d" % (_name, _t)] = ("sbuf", [128, _w], _d)
 
-ONCE = ["ldx", "ldm", "ldw", "ixt", "ihf", "gdi", "gip", "xqd", "eqd", "wqd", "qx", "oq", "mq0", "vcc", "vco", "vid",
-        "ls", "idx", "oli", "orn", "yp", "yc", "st", "sty"]
-EACH = ["sc", "rn", "ix", "ow", "oi", "pm", "ba", "bb", "bc", "bd", "nt", "nq", "ar", "ac", "os", "sl", "u1", "ab",
-        "om", "mp", "od", "nx", "on", "qp", "mc", "qc", "wi", "va", "vu", "vb", "vk", "vc", "vm", "vw"]
+ONCE = ["ldx", "ldm", "ldw", "ixt", "ihf", "gdi", "gip", "gi2", "xqd", "eqd", "wqd", "qx", "oq", "mq0", "vcc", "vco",
+        "vid", "ls", "idx", "oli", "orn", "yp", "yc", "st", "sty", "vp", "sco"]
+EACH = ["sc", "rn", "ix", "ow", "oi", "pm", "ba", "bb", "bc", "bd", "nt", "nq", "ar", "ac", "os", "sl", "sz", "u1", "ab",
+        "om", "mp", "od", "nx", "on", "oz", "qp", "mc", "qc", "wi", "va", "vu", "vb", "vk", "vc", "vm", "vw", "na", "nb",
+        "rb"]
 SEMAPHORES = ONCE + ["%s%d" % (_s, _t) for _s in EACH for _t in range(R)]
 QUARTERS = (0, 32, 64, 96)
+HALVES = (0, 64)
 
 
 def rank_program(g, core, T, topo):
@@ -74,7 +78,7 @@ def rank_program(g, core, T, topo):
 
     def wait(q, *names):
         for name in names:
-            if seen.get((q, name), 0) < total[name]:
+            if seen.get((q, name), 0) < total.get(name, 0):
                 queue[q].wait_ge(T.sem[name], total[name])
                 seen[(q, name)] = total[name]
                 seen[("", name)] = total[name]
@@ -91,28 +95,42 @@ def rank_program(g, core, T, topo):
         k = topo.chip(c)
         return (2 if topo.mates(here, k) else 1 if topo.same_plane(here, k) else 0, topo.die(c) != topo.die(core))
 
+    def partner(c):
+        return [d for d in T.cores if d != c and topo.chip(d) == topo.chip(c)][0]
+
+    def peers(c):
+        return [d for d in T.cores if topo.chip(d) != topo.chip(c) and topo.die(d) == topo.die(c)]
+
+    def slot(c, d):
+        return NQ + E * (peers(c) + peers(partner(c)) + [c, partner(c)]).index(d)
+
+    def bits(m):
+        return sum(m >> e & 1 for e in range(m.bit_length()))
+
     off = sorted([c for c in T.cores if topo.chip(c) != here], key=near)
-    on = [c for c in T.cores if c != core and topo.chip(c) == here]
+    other = partner(core)
+    same = [c for c in off if c in peers(core)]
     common = topo.mask(core, off[0])
     for c in off:
         common = common & topo.mask(core, c)
-    free = [e for e in topo.engines(core, on[0]) if not common >> e & 1]
-    local = (1 << free[0]) | (1 << free[len(free) // 2])
-    n_off = sum(common >> e & 1 for e in range(common.bit_length()))
-    arrive = len(off) * n_off + len(on) * 2
+    whole = topo.mask(core, other)
+    local = whole & ~common
 
     def dst(c):
         rid, pid = topo.addr(c)[:2]
         return DstId(rid=rid, pnc=pid)
 
-    def send(src, out, sem):
+    def send(*parts):
         g.remote_dma_fused([
-            RemoteDMATransfer(dst_ids=[dst(c) for c in off], dma_engine_mask=common, remote_sem=T.sem[sem],
-                              srcs=[src], dsts=[out for c in off]),
-            RemoteDMATransfer(dst_ids=[dst(c) for c in on], dma_engine_mask=local, remote_sem=T.sem[sem],
-                              srcs=[src], dsts=[out for c in on])], local_sem=T.sem["ls"])
-        total["ls"] = total.get("ls", 0) + n_off + 2
-        total[sem] = total.get(sem, 0) + arrive
+            RemoteDMATransfer(dst_ids=[dst(c) for c in to], dma_engine_mask=mask, remote_sem=T.sem[sem],
+                              srcs=[src], dsts=[out(c) for c in to]) for src, out, to, mask, sem in parts],
+            local_sem=T.sem["ls"])
+        for src, out, to, mask, sem in parts:
+            total["ls"] = total.get("ls", 0) + bits(mask)
+            total[sem] = total.get(sem, 0) + len(to) * bits(mask)
+
+    def spread(src, out, sem):
+        send((src, out, off, common, sem), (src, out, [other], local, sem))
 
     up(Y.dma_start(T.xt[:, 0:4 * A], T.x[:]), "ldx", 16)
     up(Y.dma_start(T.met[:], T.me[:]), "ldm", 16)
@@ -120,73 +138,69 @@ def rank_program(g, core, T, topo):
 
     up(V.memset(T.xt[:, 4 * A:512], 0.0), "ixt")
     up(V.memset(T.half[:], 0.5), "ihf")
-    up(V.memset(T.et[:], 0.0), "vcc")
     up(g.iota(T.ip[:, 0:1], [[1, 1]], 0, 1), "gip")
     up(g.iota(T.c16[:], [[16, 16]], 0, 0, allow_small_or_imprecise_dtypes=True), "gip")
-    up(g.iota(T.lp[:], [[1, 128]], 128, -1), "gip")
-    up(g.iota(T.kf[:], [[1, 32]], 0, 0, allow_small_or_imprecise_dtypes=True), "gip")
     wait("g", "ihf")
     up(g.affine_select(T.diag[:], T.half[:], [[-1, 128]], OP.is_equal, 0.0, 0, 1), "gdi")
+    wait("v", "gip")
+    up(V.tensor_scalar(T.ia[:, 0:1], T.ip[:, 0:1], 15, None, OP.bitwise_and), "vid")
+    up(V.tensor_copy(T.cst[:, 0:1], T.ip[:, 0:1]), "vp")
+    wait("v", "vid")
+    up(V.tensor_copy(T.cst[:, 1:2], T.ia[:, 0:1]), "vid")
+    up(V.memset(T.ohb[:], 0.0), "vco")
+    wait("v", "vid")
+    up(V.tensor_scalar(T.cp[:], T.c16[:], T.cst[:, 1:2], None, OP.add), "vid")
+    up(V.memset(T.slb[:], 1.0), "vco")
+    wait("v", "vid")
+    up(V.tensor_copy(T.idl[:], T.cp[:]), "vid")
+    up(V.memset(T.zz[:], 0.0), "vco")
+
     wait("v", "ldx", "ixt")
     up(V.quantize_mx(T.xq[:], T.xs[:], T.xt[:]), "xqd")
     a = A * rank
     wait("g", "xqd")
-    send(u8("xq", 0, A), u8("qa0", a, a + A), "qx")
-    send(T.xs[:, 0:A], T.qz0[:, a:a + A], "qx")
-    wait("g", "gip", "gdi")
+    send((u8("xq", 0, A), lambda c: u8("qa0", a, a + A), off, common, "qx"))
+    spread(T.xs[:, 0:A], lambda c: T.qz0[:, a:a + A], "qx")
+    send((u8("xq", 0, A), lambda c: u8("qa0", a, a + A), [other], local, "qx"))
+    up(g.iota(T.im[:], [[0, 8], [1, 16]], 0, 0, allow_small_or_imprecise_dtypes=True), "gi2")
+    up(g.iota(T.kf[:], [[1, 32]], 0, 0, allow_small_or_imprecise_dtypes=True), "gi2")
+    up(g.iota(T.rst[:], [[0, 256]], 0, 0, allow_small_or_imprecise_dtypes=True), "gi2")
+    wait("g", "gip", "gdi", "gi2")
 
-    wait("v", "gip")
-    up(V.tensor_scalar(T.ia[:, 0:1], T.ip[:, 0:1], 15, None, OP.bitwise_and), "vid")
-    up(V.tensor_copy(T.cst[:, 0:1], T.ip[:, 0:1]), "vco")
-    up(V.tensor_scalar(T.la[:], T.lp[:], 15, None, OP.bitwise_and), "vco")
-    wait("v", "vid")
-    up(V.tensor_copy(T.cst[:, 1:2], T.ia[:, 0:1]), "vid")
-    wait("v", "vid")
-    up(V.tensor_scalar(T.cp[:], T.c16[:], T.cst[:, 1:2], None, OP.add), "vid")
-    wait("v", "vid")
-    up(V.tensor_copy(T.idl[:], T.cp[:]), "vid")
+    wait("s", "vp", "vid")
+    up(S.activation(T.cst[:, 8:9], T.cst[:, 0:1], AF.Identity, bias=OUT), "sco")
+    up(S.activation(T.cst[:, 9:10], T.cst[:, 1:2], AF.Identity, bias=0.5), "sco")
+    up(S.activation(T.cst[:, 10:11], T.cst[:, 1:2], AF.Identity, bias=16.5), "sco")
+    for i, p in enumerate(HALVES):
+        up(S.activation(T.cn[p:p + 64, :], T.cp[p:p + 64, 8 * i:8 * i + 8], AF.Copy, scale=-FAR), "sco")
+    wait("s", "xqd")
+    up(S.activation(T.qz0[:, a:a + A], T.xs[:, 0:NQ].indirect(T.idl[:, 0:1]), AF.Copy), "oq")
+    for r in range(N):
+        up(S.activation(T.tab[:, r:r + 1], T.cst[:, 0:1], AF.Identity, bias=float(slot(core, T.cores[r]) - 1),
+                        scale=-1.0), "sco")
+
+    up(V.memset(T.et[:], 0.0), "vcc")
     wait("v", "vid", "xqd")
     up(V.tensor_copy(u32("qa0", a, a + A), u32("xq", 0, NQ).indirect(T.idl[:, 0:1])), "oq")
-    wait("s", "vid", "xqd")
-    up(S.activation(T.qz0[:, a:a + A], T.xs[:, 0:NQ].indirect(T.idl[:, 0:1]), AF.Copy), "oq")
     wait("v", "vcc", "gdi")
     for b in range(4):
         up(V.tensor_copy(T.et[:, 512 * b + b:512 * b + 512:4], T.diag[:]), "vcc")
-    up(V.memset(T.zz[:], 0.0), "vco")
-    wait("v", "vcc")
-    up(V.quantize_mx(T.eq[:], T.ez[:], T.et[:]), "eqd")
     wait("v", "ldm")
     up(V.quantize_mx(T.mq0[:], T.mz0[:], T.met[:]), "mq0")
-    up(V.memset(T.rst[:], -BIG), "vco")
+    wait("v", "vcc")
+    up(V.quantize_mx(T.eq[:], T.ez[:], T.et[:]), "eqd")
+    up(V.quantize_mx(T.mw0[:, E:E + M], T.mx0[:, E:E + M], T.met[:]), "mc0")
     for t in range(R):
-        o = AT["oh"][0]
-        up(V.memset(T["f%d" % t][:, o:o + 32], 0.0), "vco")
-        o = AT["sl"][0]
-        up(V.memset(T["f%d" % t][:, o:o + 1], 1.0), "vco")
-        up(V.memset(T["ri%d" % t][:], 1000.0), "vco")
+        up(V.memset(T["ri%d" % t][:, NQ:RI], 1000.0 * FAR), "vco")
         up(V.memset(T["nt%d" % t][:, 512:520], 0.0), "vco")
-    up(V.tensor_scalar(T.kq[:], T.kf[:], 1.0 / 64, None, OP.mult), "vco")
-    up(V.tensor_copy(T.cc[0:32, :], T.cp[0:32, 0:8]), "vco")
-    up(V.tensor_copy(T.cc[32:64, :], T.cp[32:64, 8:16]), "vco")
-    wait("v", "mq0")
-    up(V.tensor_copy(u32("mw0", 0, M), u32("mq0", 0, M).indirect(T.idl[:])), "mc0")
-    wait("s", "mq0")
-    up(S.activation(T.mx0[:, 0:M], T.mz0[:].indirect(T.idl[:]), AF.Copy), "mc0")
-    wait("v", "vco")
-    up(V.memset(T.rst[:, 0:256:32], BIG), "vco")
-    up(V.tensor_scalar(T.wm[:], T.la[:, 0:32], 0, None, OP.is_equal), "vco")
-    up(V.tensor_scalar(T.nwm[:], T.la[:], 0, None, OP.not_equal), "vco")
-    up(V.tensor_scalar(T.cst[:, 2:3], T.cst[:, 0:1], -1.0, float(NQ - 1), OP.mult, OP.add), "vco")
-    up(V.tensor_scalar(T.cst[:, 3:4], T.cst[:, 0:1], OUT, None, OP.add), "vco")
-    up(V.tensor_scalar(T.cst[:, 4:5], T.cst[:, 1:2], 0.5, None, OP.add), "vco")
-    up(V.tensor_scalar(T.cst[:, 5:6], T.cst[:, 1:2], 16.5, None, OP.add), "vco")
-    up(V.tensor_scalar(T.cn[0:64, :], T.cc[0:64, :], -1.0, None, OP.mult), "vco")
-    wait("v", "vco")
-    up(V.tensor_scalar(T.wp[:], T.wm[:], T.cst[:, 3:4], -OUT, OP.mult, OP.add), "vco")
-    wait("v", "ldw")
-    up(V.quantize_mx(T.wq[:], T.wz[:], T.wt[:]), "wqd")
-    wait("v", "vco")
-    wait("s", "vco")
+    wait("v", "gi2")
+    up(V.tensor_scalar(T.wm[:], T.im[:, 0:32], T.cst[:, 1:2], None, OP.is_equal), "vco")
+    up(V.tensor_scalar(T.nwm[:], T.im[:], T.cst[:, 1:2], None, OP.not_equal), "vco")
+    for i, p in enumerate(HALVES):
+        up(V.tensor_scalar(T.rst[p:p + 64, 0:256:32], T.cp[p:p + 64, 8 * i:8 * i + 8], float(E), None, OP.add), "vco")
+    wait("v", "vco", "sco")
+    up(V.tensor_scalar(T.wp[:], T.wm[:], T.cst[:, 8:9], -OUT, OP.mult, OP.add), "vco")
+    wait("s", "sco")
 
     for t in range(R):
         def B(name, u=t):
@@ -203,27 +217,38 @@ def rank_program(g, core, T, topo):
             o, w = AT[name]
             return B("f")[p:p + n, o + a:o + (w if b is None else b):step]
 
+        def sl(a, b):
+            return T.slb[:, 16 * t + a:16 * t + b]
+
+        def oh(u=t):
+            return T.ohb[:, 32 * u:32 * u + 8]
+
         def fold(row, block, sem):
             for p in QUARTERS:
-                up(V.transpose(row[0:32, p:p + 32], h(block, p=p)), sem)
+                up(V.transpose(row[0:32, p:p + 32], block[p:p + 32, :]), sem)
 
         def lanes(out, y, sem):
             for p in QUARTERS:
                 up(V.tensor_copy(out[p:p + 32, 0:8], h(y, 15, 128, 16)), sem)
+
+        def whole_of(name, rows=slice(0, 128)):
+            o, w = AT[name]
+            return lambda r, c: B("f")[r, o + c.start:o + c.stop]
 
         def number(step, u=t):
             where = T.land1[:, 1:32:4] if u == 0 else T.lidx[:, 0:32:4]
             one, vw = (0, 1, 1, u), s("vw", u)
             wait("v", vw)
             if step == 0:
-                up(V.tensor_tensor(f("ol", 0, 8, 1, u), f("oh", 0, 8, 1, u), where, OP.mult), vw)
+                up(V.tensor_tensor(f("ol", 0, 8, 1, u), oh(u), where, OP.mult), vw)
             elif step == 1:
                 up(V.tensor_reduce(f("ix", *one), f("ol", 0, 8, 1, u), AX, OP.add), vw)
-            elif step == 2:
-                up(V.tensor_scalar(f("gg", *one), f("tw", *one), float(M), f("ix", *one), OP.mult, OP.add), vw)
             else:
-                up(V.tensor_scalar(B("wv", u)[:, 0:1], f("gg", *one), f("b2", *one), f("b1", *one), OP.mult, OP.add),
-                   s("wi", u))
+                up(V.tensor_scalar(B("wv", u)[:, 0:1], f("ix", *one), f("b2", *one), -0.5, OP.mult, OP.add), s("wi", u))
+
+        def turn(row, block, sem):
+            for p in QUARTERS:
+                up(V.transpose(h(row, p, p + 32), h(block, p=p)), sem)
 
         one = (0, 1)
         va, vu, vb, vk, vc, vm = s("va"), s("vu"), s("vb"), s("vk"), s("vc"), s("vm")
@@ -236,7 +261,7 @@ def rank_program(g, core, T, topo):
         wait("t", "eqd")
         if t:
             wait("t", s("nt", 0))
-        for b in (0, 2, 1, 3):
+        for b in (0, 1, 2, 3):
             P.matmul_mx(T.pbl[:, 512 * b:512 * b + NQ], T.eq[:, 128 * b:128 * b + 128], T.ez[:, 128 * b:128 * b + 128],
                         qa[:], qz[:], True, False)
         run, land, k = B("run"), B("land"), 4 * rank
@@ -244,31 +269,38 @@ def rank_program(g, core, T, topo):
         up(V.tensor_tensor_scan(run[:, 0:M], T.psc[:, 0:M], T.zz[:], LOW, OP.max, OP.add), s("rn"))
         wait("g", s("rn"))
         if t == 0:
-            send(run[:, M - 1:M], land[:, k:k + 1], s("ar"))
+            spread(run[:, M - 1:M], lambda c: land[:, k:k + 1], s("ar"))
         else:
             wait("g", "orn")
-            send(run[:, M - 1:M + 1], land[:, k:k + 2], s("ar"))
+            spread(run[:, M - 1:M + 1], lambda c: land[:, k:k + 2], s("ar"))
         wait("s", s("rn"))
         up(S.activation(f("sg"), run[:, 0:M], AF.Sign, bias=run[:, M - 1:M], scale=-1.0, accum_out=f("ti", *one)), s("ix"))
         up(S.activation(land[:, k:k + 1], run[:, M - 1:M], AF.Copy), s("ow"))
+        wait("s", s("ix"))
+        base = M * rank + 0.5
         if t == 0:
-            wait("v", "oq", "qx")
+            up(S.activation(T.run1[:, M:M + 1], f("ti", *one), AF.Identity, bias=base), "orn")
+            up(S.activation(T.land1[:, k + 1:k + 2], f("ti", *one), AF.Identity, bias=base), "orn")
+        else:
+            up(S.activation(T.lidx[:, k:k + 1], f("ti", *one), AF.Identity, bias=base), "oli")
+        if t == 0:
+            wait("v", "oq", "qx", "vco")
             wait("s", "oq", "qx")
             up(V.tensor_copy(u32("win0", 0, NQ), u32("qa0", 0, NQ).indirect(T.idl[:, 0:8])), s("qc"))
             up(S.activation(T.wis0[:, 0:NQ], T.qz0[:, 0:NQ].indirect(T.idl[:, 0:8]), AF.Copy), s("qc"))
         else:
             up(V.tensor_copy(u32("win1", 0, NQ), u32("win0", 0, NQ + N * E).indirect(T.offq0[:, 0:8])), s("qc"))
             up(S.activation(T.wis1[:, 0:NQ], T.wis0[:, 0:NQ + N * E].indirect(T.offq0[:, 0:8]), AF.Copy), s("qc"))
-            wait("g", s("ix"))
-            send(f("ti", *one), T.lidx[:, k:k + 1], "idx")
+            wait("g", "oli")
+            spread(T.lidx[:, k:k + 1], lambda c: T.lidx[:, k:k + 1], "idx")
             wait("y", s("mp", 0), s("ar"))
-            up(Y.dma_start(u8("mw1", 0, M), u8("mq1", 0, M)), "mc1", 16)
-            up(Y.dma_start(T.mx1[:, 0:M], T.mz1[:]), "mc1", 16)
+            up(Y.dma_start(u8("mw1", E, E + M), u8("mq1", 0, M)), "mc1", 16)
+            up(Y.dma_start(T.mx1[:, E:E + M], T.mz1[:]), "mc1", 16)
         wait("v", s("ix"))
         up(V.tensor_scalar(f("ra"), T.wm[:], f("ti", *one), None, OP.mult), va)
-        up(V.tensor_scalar(f("ru"), T.zz[:, 0:32], f("ti", *one), None, OP.add), vu)
+        up(V.tensor_scalar(f("ru"), T.zz[:, 0:32], f("ti", *one), FAR, OP.add, OP.mult), vu)
         wait("v", va)
-        fold(f("la"), "ra", va)
+        turn("la", "ra", va)
         wait("v", va)
         up(V.tensor_tensor_scan(h("ly"), T.nwm[0:32, :], h("la"), 0.0, OP.mult, OP.add), va)
         wait("v", va)
@@ -279,75 +311,76 @@ def rank_program(g, core, T, topo):
         up(S.activation(B("pz")[:, 0:NQ], mz[:, 0:M].indirect(B("offi")[:, 0:8]), AF.Copy), s("pm"))
         ri = B("ri")
         wait("v", vu)
-        fold(ri, "ru", vu)
+        turn("rr", "ru", vu)
+        wait("g", vu)
+        up(g.partition_broadcast(ri[:, 0:NQ], h("rr", n=1), 128), s("rb"))
         wait("t", s("pm"))
         bank = {0: s("ba"), 1: s("bb"), 2: s("bc"), 3: s("bd")}
-        for b in (0, 2, 1, 3):
+        for b in (0, 1, 2, 3):
             up(P.matmul_mx(T.pbl[:, 512 * b:512 * b + NQ], T.eq[:, 128 * b:128 * b + 128], T.ez[:, 128 * b:128 * b + 128],
                            B("pm")[:], B("pz")[:], False, True), bank[b])
         nt = B("nt")
-        for b in (0, 1):
-            wait("v", bank[b])
-            up(V.tensor_copy(nt[:, b:512:4], T.pbl[:, 512 * b:512 * b + NQ]), s("nt"))
-        for b in (2, 3):
+        wait("v", bank[0])
+        up(V.tensor_copy(nt[:, 0:512:4], T.pbl[:, 0:NQ]), s("nt"))
+        for b in (1, 2, 3):
             wait("s", bank[b])
             up(S.activation(nt[:, b:512:4], T.pbl[:, 512 * b:512 * b + NQ], AF.Copy), s("nt"))
-        wait("v", s("nt"))
-        up(V.quantize_mx(B("nq")[:, 0:130], B("nz")[:, 0:130], nt[:]), s("nq"))
-        wait("v", vu)
-        up(V.tensor_copy(ri[32:64, 0:NQ], ri[0:32, 0:NQ]), vu)
-        wait("s", s("ix"))
-        if t == 0:
-            up(S.activation(T.run1[:, M:M + 1], f("ti", *one), AF.Copy), "orn")
-            up(S.activation(T.land1[:, k + 1:k + 2], f("ti", *one), AF.Copy), "orn")
-        else:
-            up(S.activation(T.lidx[:, k:k + 1], f("ti", *one), AF.Copy), "oli")
         wait("v", s("ow"), s("ar"))
         up(V.tensor_tensor_scan(f("rl"), land[:, 0:32:4], T.zz[:, 0:8], LOW, OP.max, OP.add), vb)
         wait("v", vb)
-        up(V.tensor_scalar(f("sl", 1, 9), f("rl"), f("rl", 7, 8), None, OP.is_lt), vb)
+        up(V.tensor_scalar(sl(1, 9), f("rl"), f("rl", 7, 8), None, OP.is_lt), vb)
         wait("v", vb)
-        up(V.tensor_scalar(f("fr"), T.zz[:, 0:32], f("sl", rank, rank + 1), f("sl", rank + 1, rank + 2), OP.add,
-                           OP.subtract), vb)
-        up(V.tensor_tensor(f("oh", 0, 8), f("sl", 0, 8), f("sl", 1, 9), OP.subtract), vc)
+        up(V.tensor_scalar(f("fr"), T.zz[:, 0:32], sl(rank, rank + 1), sl(rank + 1, rank + 2), OP.add, OP.subtract), vb)
+        up(V.tensor_tensor(oh(), sl(0, 8), sl(1, 9), OP.subtract), vc)
         wait("v", vb)
-        fold(f("ft"), "fr", vb)
-        up(V.tensor_reduce(f("tw", *one), f("sl", 1, 9), AX, OP.add), vk)
+        turn("ft", "fr", vb)
         wait("v", vb)
         up(V.tensor_tensor_scan(h("cn"), h("ft"), T.zz[0:32, 0:128], 0.0, OP.add, OP.add), vb)
         wait("s", vb)
-        up(S.activation(h("sa"), h("cn"), AF.Sign, bias=T.cst[0:32, 4:5], scale=-1.0, accum_out=h("acc", 0, 1)), s("ac"))
-        up(S.activation(h("sb"), h("cn"), AF.Sign, bias=T.cst[0:32, 5:6], scale=-1.0, accum_out=h("acc", 1, 2)), s("ac"))
+        up(S.activation(h("sa"), h("cn"), AF.Sign, bias=T.cst[0:32, 9:10], scale=-1.0, accum_out=h("acc", 0, 1)), s("ac"))
+        up(S.activation(h("sb"), h("cn"), AF.Sign, bias=T.cst[0:32, 10:11], scale=-1.0, accum_out=h("acc", 1, 2)), s("ac"))
         wait("v", vc)
-        fold(f("ot"), "oh", vc)
-        wait("v", vc)
-        up(V.tensor_tensor_scan(h("ct"), h("ot"), T.zz[0:32, 0:128], 0.0, OP.add, OP.add), vc)
-        wait("v", s("ac"), s("nq"))
+        for p in QUARTERS:
+            up(V.transpose(h("ot", p, p + 32), T.ohb[p:p + 32, 32 * t:32 * t + 32]), vc)
+        wait("v", s("nt"))
+        up(V.quantize_mx(B("nq")[:, 0:130], B("nz")[:, 0:130], nt[:]), s("nq"))
+        wait("v", s("ac"))
         offs = B("offs")
         for p in QUARTERS:
             up(V.tensor_scalar(offs[p:p + 32, 0:2], h("acc", 0, 2), 0.5, 64.0, OP.mult, OP.add), s("os"))
-        wait("v", s("os"))
-        up(V.tensor_copy(u32(s("mw"), M, M + E), u32(s("nq"), 0, 130).indirect(offs[:, 0:2])), s("sl"))
+        wait("v", s("os"), s("nq"))
+        up(V.tensor_copy(u32(s("mw"), 0, E), u32(s("nq"), 0, 130).indirect(offs[:, 0:2])), s("sl"))
         wait("s", s("nq"), s("os"))
-        up(S.activation(B("mx")[:, M:M + E], B("nz")[:, 0:130].indirect(offs[:, 0:2]), AF.Copy), s("sl"))
+        up(S.activation(B("mx")[:, 0:E], B("nz")[:, 0:130].indirect(offs[:, 0:2]), AF.Copy), s("sz"))
+
+        def codes(c):
+            return u8(s("win"), slot(c, core), slot(c, core) + E)
+
         wait("g", s("sl"))
-        e = NQ + E * rank
-        send(u8(s("mw"), M, M + E), u8(s("win"), e, e + E), s("nx"))
-        send(B("mx")[:, M:M + E], B("wis")[:, e:e + E], s("nx"))
-        wait("v", vu)
-        up(V.tensor_tensor(B("uu")[:, 0:E], ri[:, 0:136].indirect(offs[:, 0:2]), T.kq[:], OP.add), s("u1"))
+        send((u8(s("mw"), 0, E), codes, same, common, s("na")), (u8(s("mw"), 0, E), codes, [other], local, s("nx")))
+        wait("g", s("sz"))
+        spread(B("mx")[:, 0:E], lambda c: B("wis")[:, slot(c, core):slot(c, core) + E], s("nb"))
+        wait("g", s("na"))
+        n = E * len(same)
+        send((u8(s("win"), NQ, NQ + n), lambda c: u8(s("win"), NQ + n, NQ + 2 * n), [other], whole, s("nx")))
+        e = slot(core, core)
+        wait("v", s("rb"))
+        up(V.tensor_tensor(B("uu")[:, 0:E], ri[:, 0:RI].indirect(offs[:, 0:2]), T.kf[:], OP.add), s("u1"))
         wait("s", s("u1"))
         for c in range(8):
-            up(S.activation(h("ab", 32 * c, 32 * c + 32, n=64), B("uu")[0:64, 0:E], AF.Abs, bias=T.cn[0:64, c:c + 1],
-                            scale=1.0), s("ab"))
-        up(S.activation(B("wis")[:, e:e + E], B("nz")[:, 0:130].indirect(offs[:, 0:2]), AF.Copy), s("on"))
+            up(S.activation(f("ab", 32 * c, 32 * c + 32), B("uu")[:, 0:E], AF.Abs, bias=T.cn[:, c:c + 1], scale=1.0),
+               s("ab"))
+        up(S.activation(B("wis")[:, e:e + E], B("nz")[:, 0:130].indirect(offs[:, 0:2]), AF.Copy), s("oz"))
+        wait("v", vc)
+        up(V.tensor_tensor_scan(h("ct"), h("ot"), T.zz[0:32, 0:128], 0.0, OP.add, OP.add), vc)
+        up(V.tensor_tensor(f("t0"), T.tab[:], oh(), OP.mult), vk)
         wait("v", vc)
         for p in QUARTERS:
             up(V.transpose(h("cb", p=p), h("ct", p, p + 32)), vc)
         wait("v", vk)
-        up(V.tensor_scalar(f("t1", *one), f("tw", *one), float(E), T.cst[:, 2:3], OP.mult, OP.add), vk)
+        up(V.tensor_reduce(f("t1", *one), f("t0"), AX, OP.add), vk)
         wait("v", vc)
-        up(V.tensor_tensor(f("kr"), f("cb", 0, 8), f("oh", 0, 8), OP.mult), vc)
+        up(V.tensor_tensor(f("kr"), f("cb", 0, 8), oh(), OP.mult), vc)
         up(V.tensor_copy(u32(s("win"), e, e + E), u32(s("nq"), 0, 130).indirect(offs[:, 0:2])), s("on"))
         wait("v", vc)
         up(V.tensor_reduce(f("kk", *one), f("kr"), AX, OP.add), vc)
@@ -361,58 +394,48 @@ def rank_program(g, core, T, topo):
         wait("v", vc, vk)
         up(V.tensor_scalar(f("tt", *one), f("kk", *one), f("t1", *one), f("an", *one), OP.add, OP.mult), vc)
         up(V.tensor_scalar(f("b2", *one), f("an", *one), 2.0, -1.0, OP.mult, OP.add), s("vw"))
-        up(V.tensor_scalar(f("b1", *one), f("an", *one), -1.0, None, OP.add), s("vw"))
         wait("v", vc)
         up(V.tensor_scalar(f("rc"), T.wp[:], f("tt", *one), 0.0, OP.add, OP.max), vc)
         if t:
             number(2, 0)
         wait("v", vc)
-        fold(f("lc"), "rc", vc)
-        if t:
-            number(3, 0)
-        wait("v", s("ab"))
-        up(V.tensor_tensor_scan(h("am", n=64), T.rst[0:64, :], h("ab", n=64), 0.0, OP.max, OP.min), vm)
+        turn("lc", "rc", vc)
         wait("v", vc)
         up(V.tensor_tensor_scan(h("oy"), T.nwm[0:32, :], h("lc"), 0.0, OP.mult, OP.add), vc)
-        wait("v", vm)
-        low = h("am", 31, 256, 32, n=64)
-        up(V.tensor_scalar(h("m1", n=64), low, 0.5, None, OP.is_lt), vm)
-        up(V.tensor_scalar(h("m2", n=64), low, 64.0, float(M), OP.mult, OP.add), vm)
-        if t:
-            wait("v", "idx", "oli")
-            number(0, 1)
-        wait("v", vm)
-        up(V.tensor_tensor(h("m3", n=64), h("m1", n=64), h("m2", n=64), OP.mult), vm)
-        if t:
-            number(1, 1)
-        wait("v", vm)
-        up(V.tensor_tensor(h("m4", n=64), h("m3", n=64), T.cc[0:64, :], OP.max), vm)
+        wait("v", s("ab"))
+        up(V.tensor_tensor_scan(f("am"), T.rst[:], f("ab"), 0.0, OP.max, OP.min), vm)
         wait("v", vc)
         lanes(B("offq"), "oy", s("od"))
         wait("v", vm)
-        for p in QUARTERS:
-            up(V.tensor_copy(B("offm")[p:p + 32, 0:8], h("m4")), s("om"))
-            up(V.tensor_copy(B("offm")[p:p + 32, 8:16], h("m4", p=32)), s("om"))
+        for p in HALVES:
+            for i, q in enumerate(HALVES):
+                up(V.tensor_copy(B("offm")[p:p + 64, 8 * i:8 * i + 8], h("am", 31, 256, 32, p=q, n=64)), s("om"))
         if t:
-            number(2, 1)
-            number(3, 1)
+            wait("v", "idx", "oli")
+            number(0, 1)
+        else:
+            wait("v", "ldw")
+            up(V.quantize_mx(T.wq[:], T.wz[:], T.wt[:]), "wqd")
         wait("v", s("om"), s("sl"), s("mc"))
         mp = s("mp")
         up(V.tensor_copy(u32(s("mq", t + 1), 0, M), u32(s("mw"), 0, M + E).indirect(B("offm")[:, 0:16])), mp)
-        wait("s", s("om"), s("sl"), s("mc"))
+        wait("s", s("om"), s("sz"), s("mc"))
         up(S.activation(B("mz", t + 1)[:, 0:M], B("mx")[:, 0:M + E].indirect(B("offm")[:, 0:16]), AF.Copy), mp)
-        for q in ("v", "s"):
-            wait(q, s("od"), s("on"), s("qc"), s("nx"))
+        if t:
+            number(1, 1)
+            number(2, 1)
+        wait("v", s("od"), s("on"), s("qc"), s("na"), s("nx"))
+        wait("s", s("od"), s("oz"), s("qc"), s("nb"))
         up(V.tensor_copy(u32(s("qa", t + 1), 0, NQ), u32(s("win"), 0, NQ + N * E).indirect(B("offq")[:, 0:8])), s("qp"))
         up(S.activation(B("qz", t + 1)[:, 0:NQ], B("wis")[:, 0:NQ + N * E].indirect(B("offq")[:, 0:8]), AF.Copy), s("qp"))
 
-    wait("y", "wi0", "wi1")
-    for u in range(R):
-        up(Y.dma_start(T.wi[u:u + 1, :], T["wv%d" % u][:, 0:1]), "st", 16)
-    wait("y", "mp1", "nx1")
+    wait("y", "mp1", "nx1", "nb1")
     up(Y.dma_start(T.oc[:, 0:4 * M], u8("mq%d" % R, 0, M)), "st", 16)
     for c in range(4):
         up(Y.dma_start(T.osc[4 * c:4 * c + 4, 0:M], T["mz%d" % R][32 * c:32 * c + 4, 0:M]), "st", 16)
+    wait("y", "wi0", "wi1")
+    for u in range(R):
+        up(Y.dma_start(T.wi[u:u + 1, :], T["wv%d" % u][:, 0:1]), "st", 16)
     wait("t", "wqd", "qp1")
     up(P.matmul_mx(T.pyy[:, 0:NQ], T.wq[:], T.wz[:], T.qa2[:], T.qz2[:], True, True), "yp")
     wait("v", "yp")

@@ -3,41 +3,47 @@ from concourse.mybir import dt, AluOpType, AxisListType, ActivationFunctionType
 
 N, M, A, E, R = 8, 256, 16, 32, 2
 NQ = N * A
+NS = N * E
+H = M // 2
 OP = AluOpType
 AF = ActivationFunctionType
 AX = AxisListType.X
 LOW = -9.0e29
-OUT = 65536.0
-FAR = 512.0
-
-WORK = [("ti", 8), ("ra", 32), ("ru", 32), ("fr", 32), ("cb", 32), ("rc", 32), ("la", 128), ("rr", 128),
-        ("ly", 128), ("ft", 128), ("cn", 128), ("sa", 128), ("sb", 128), ("acc", 8), ("ot", 128), ("ct", 128), ("lc", 128),
-        ("oy", 128), ("rl", 8), ("t0", 8), ("t1", 8), ("kr", 8), ("kk", 8), ("an", 8), ("tt", 8),
-        ("ol", 8), ("ix", 8), ("b2", 8), ("sg", 256), ("ab", 256), ("am", 256)]
-AT = {}
-_n = 0
-for _name, _w in WORK:
-    AT[_name] = (_n, _w)
-    _n += _w
+FAR = 1024.0
+WON = -256.0
+NB = 160
+MW = R * NB + M
 RI = NQ + 8
+
+WORK = [("ti", 8), ("acc", 8), ("rl", 8), ("kk", 16), ("ol", 8), ("ix", 8), ("b2", 8),
+        ("sg", 256), ("ab", 256), ("am", 256)]
+HALF = [("ra", 32), ("la", 128), ("ly", 128), ("wn", 48), ("fr", 48), ("ft", 128), ("sa", 128), ("sb", 128),
+        ("oh", 16), ("dd", 32), ("ot", 128), ("ct", 128), ("cb", 48), ("sl", 16), ("rc", 32), ("lc", 128), ("oy", 128)]
+AT = {}
+_n = {}
+for _b, _l in (("f", WORK), ("h", HALF)):
+    _n[_b] = 0
+    for _name, _w in _l:
+        AT[_name] = (_b, _n[_b], _w)
+        _n[_b] += _w
 
 SCRATCH = {
     "xt": ("sbuf", [128, 512], "bfloat16"), "met": ("sbuf", [128, 4 * M], "bfloat16"),
-    "wt": ("sbuf", [128, 512], "bfloat16"), "et": ("sbuf", [128, 2048], "bfloat16"),
+    "wt": ("sbuf", [128, 512], "bfloat16"), "et": ("sbuf", [128, 520], "bfloat16"),
     "half": ("sbuf", [128, 128], "bfloat16"), "diag": ("sbuf", [128, 128], "bfloat16"),
-    "xq": ("sbuf", [128, 128], "float8_e4m3fn_x4"), "xs": ("sbuf", [128, 128], "uint8"),
+    "xq": ("sbuf", [128, 160], "float8_e4m3fn_x4"), "xs": ("sbuf", [128, 160], "uint8"),
     "wq": ("sbuf", [128, 128], "float8_e4m3fn_x4"), "wz": ("sbuf", [128, 128], "uint8"),
     "eq": ("sbuf", [128, 512], "float8_e4m3fn_x4"), "ez": ("sbuf", [128, 512], "uint8"),
-    "zz": ("sbuf", [128, 256], "float32"), "wm": ("sbuf", [128, 32], "float32"), "nwm": ("sbuf", [128, 128], "float32"),
-    "wp": ("sbuf", [128, 32], "float32"), "tab": ("sbuf", [128, 8], "float32"),
-    "rst": ("sbuf", [128, 256], "float32"), "im": ("sbuf", [128, 128], "float32"),
-    "ip": ("sbuf", [128, 8], "int32"), "ia": ("sbuf", [128, 8], "int32"), "kf": ("sbuf", [128, 32], "float32"),
+    "zz": ("sbuf", [128, 128], "bfloat16"), "one": ("sbuf", [128, 128], "bfloat16"),
+    "wm": ("sbuf", [128, 32], "bfloat16"), "nwm": ("sbuf", [128, 128], "bfloat16"),
+    "wp": ("sbuf", [128, 32], "bfloat16"), "old": ("sbuf", [128, 128], "bfloat16"), "tb": ("sbuf", [128, 16], "float32"),
+    "rst": ("sbuf", [128, 256], "float32"), "im": ("sbuf", [128, 128], "float32"), "pl": ("sbuf", [128, M], "float32"),
+    "ip": ("sbuf", [128, 8], "int32"), "ia": ("sbuf", [128, 8], "int32"), "jr": ("sbuf", [128, R * NQ], "float32"),
     "c16": ("sbuf", [128, 16], "float32"), "cp": ("sbuf", [128, 16], "float32"),
-    "cn": ("sbuf", [128, 8], "float32"), "ohb": ("sbuf", [128, 32 * R], "float32"),
-    "slb": ("sbuf", [128, 16 * R], "float32"),
+    "cn": ("sbuf", [128, 8], "float32"),
     "cst": ("sbuf", [128, 32], "float32"), "yt": ("sbuf", [128, 128], "float32"),
-    "idl": ("sbuf", [128, 16], "uint16"), "lidx": ("sbuf", [128, 32], "float32"),
-    "psc": ("psum", [128, 512], "float32"), "pbl": ("psum", [128, 2048], "float32"), "pyy": ("psum", [128, 512], "float32"),
+    "idl": ("sbuf", [128, 16], "uint16"),
+    "psc": ("psum", [128, 1024], "float32"), "pbl": ("psum", [128, 2048], "float32"), "pyy": ("psum", [128, 512], "float32"),
 }
 for _t in range(R + 1):
     SCRATCH["mq%d" % _t] = ("sbuf", [128, M], "float8_e4m3fn_x4")
@@ -45,36 +51,54 @@ for _t in range(R + 1):
     SCRATCH["qa%d" % _t] = ("sbuf", [128, NQ], "float8_e4m3fn_x4")
     SCRATCH["qz%d" % _t] = ("sbuf", [128, NQ], "uint8")
 for _t in range(R):
-    for _name, _w, _d in (("mw", M + E, "float8_e4m3fn_x4"), ("mx", M + E, "uint8"),
-                          ("win", NQ + N * E, "float8_e4m3fn_x4"), ("wis", NQ + N * E, "uint8"),
+    for _name, _w, _d in (("mw", MW, "float8_e4m3fn_x4"), ("mx", MW, "uint8"),
+                          ("win", NS + NQ, "float8_e4m3fn_x4"), ("wis", NS + NQ, "uint8"),
                           ("pm", NQ, "float8_e4m3fn_x4"), ("pz", NQ, "uint8"),
-                          ("nq", 160, "float8_e4m3fn_x4"), ("nz", 160, "uint8"),
-                          ("nt", 520, "bfloat16"), ("run", 264, "float32"), ("land", 32, "float32"),
-                          ("ri", RI, "float32"), ("uu", 32, "float32"), ("wv", 8, "float32"), ("f", _n, "float32"),
+                          ("nt", 520, "bfloat16"), ("run", M, "float32"), ("land", 32, "float32"), ("num", 32, "float32"),
+                          ("ri", RI, "float32"), ("wv", 8, "float32"),
+                          ("f", _n["f"], "float32"), ("h", _n["h"], "bfloat16"),
                           ("offi", 8, "uint16"), ("offs", 2, "uint16"), ("offm", 16, "uint16"), ("offq", 8, "uint16")):
         SCRATCH["%s%d" % (_name, _t)] = ("sbuf", [128, _w], _d)
 
-ONCE = ["ldx", "ldm", "ldw", "ixt", "ihf", "gdi", "gip", "gi2", "xqd", "eqd", "wqd", "qx", "oq", "mq0", "vcc", "vco",
-        "vid", "ls", "idx", "oli", "orn", "yp", "yc", "st", "sty", "vp", "sco"]
-EACH = ["sc", "rn", "ix", "ow", "oi", "pm", "ba", "bb", "bc", "bd", "nt", "nq", "ar", "ac", "os", "sl", "sz", "u1", "ab",
-        "om", "mp", "od", "nx", "on", "oz", "qp", "mc", "qc", "wi", "va", "vu", "vb", "vk", "vc", "vm", "vw", "na", "nb",
-        "rb"]
+ONCE = ["ldx", "ldm", "ldw", "ixt", "ihf", "gdi", "gip", "gi1", "gi2", "xqd", "eqd", "wqd", "qx", "px", "oq", "op", "mq0",
+        "vcc", "vco", "vid", "ls", "yp", "yc", "st", "sty", "sco", "rs"]
+EACH = ["sa", "sb", "ra", "rn", "ix", "ow", "oi", "pm", "ba", "bb", "bc", "bd", "nt", "nq", "ar", "ac", "os", "sl", "sz",
+        "ab", "om", "mp", "mo", "od", "nx", "qp", "qc", "wi", "va", "vb", "vk", "vc", "vm", "vw", "na",
+        "nb", "rb", "ni", "id", "vr", "m2", "mc"]
 SEMAPHORES = ONCE + ["%s%d" % (_s, _t) for _s in EACH for _t in range(R)]
 QUARTERS = (0, 32, 64, 96)
 HALVES = (0, 64)
 
 
 def rank_program(g, core, T, topo):
+    def partner(c):
+        return [d for d in T.cores if d != c and topo.chip(d) == topo.chip(c)][0]
+
+    def helpers(c):
+        idle = [d for d in topo.cores_of(c) if d not in T.cores and topo.die(d) == topo.die(c)]
+        port = [d for d in idle if all(topo.may_write(d, r) for r in T.cores)][0]
+        return [port, [d for d in idle if d != port][0]]
+
+    def slot(d):
+        return NS - E * (T.rank_of(d) + 1)
+
+    def bits(m):
+        return sum(m >> e & 1 for e in range(m.bit_length()))
+
     rank = T.rank_of(core)
-    if rank is None:
+    served = [c for c in T.cores if core in helpers(c)]
+    if rank is None and not served:
         return
     V, S, P, Y = g.vector, g.scalar, g.tensor, g.sync
     queue = {"v": V, "s": S, "t": P, "y": Y, "g": g}
     total, seen = {}, {}
 
+    def comes(name, n):
+        total[name] = total.get(name, 0) + n
+
     def up(ins, name, n=1):
         ins.then_inc(T.sem[name], n)
-        total[name] = total.get(name, 0) + n
+        comes(name, n)
 
     def wait(q, *names):
         for name in names:
@@ -82,6 +106,11 @@ def rank_program(g, core, T, topo):
                 queue[q].wait_ge(T.sem[name], total[name])
                 seen[(q, name)] = total[name]
                 seen[("", name)] = total[name]
+
+    def rest():
+        for name in total:
+            if seen.get(("", name), 0) < total[name]:
+                wait("g", name)
 
     def u32(name, a, b):
         return T[name][:, a:b].bitcast(dt.uint32)
@@ -95,26 +124,13 @@ def rank_program(g, core, T, topo):
         k = topo.chip(c)
         return (2 if topo.mates(here, k) else 1 if topo.same_plane(here, k) else 0, topo.die(c) != topo.die(core))
 
-    def partner(c):
-        return [d for d in T.cores if d != c and topo.chip(d) == topo.chip(c)][0]
-
-    def peers(c):
-        return [d for d in T.cores if topo.chip(d) != topo.chip(c) and topo.die(d) == topo.die(c)]
-
-    def slot(c, d):
-        return NQ + E * (peers(c) + peers(partner(c)) + [c, partner(c)]).index(d)
-
-    def bits(m):
-        return sum(m >> e & 1 for e in range(m.bit_length()))
-
     off = sorted([c for c in T.cores if topo.chip(c) != here], key=near)
-    other = partner(core)
-    same = [c for c in off if c in peers(core)]
+    far, plane, mates = [[c for c in off if near(c)[0] == i] for i in range(3)]
+    same = [c for c in off if topo.die(c) == topo.die(core)]
     common = topo.mask(core, off[0])
     for c in off:
         common = common & topo.mask(core, c)
-    whole = topo.mask(core, other)
-    local = whole & ~common
+    wide = bits(common)
 
     def dst(c):
         rid, pid = topo.addr(c)[:2]
@@ -123,84 +139,115 @@ def rank_program(g, core, T, topo):
     def send(*parts):
         g.remote_dma_fused([
             RemoteDMATransfer(dst_ids=[dst(c) for c in to], dma_engine_mask=mask, remote_sem=T.sem[sem],
-                              srcs=[src], dsts=[out(c) for c in to]) for src, out, to, mask, sem in parts],
+                              srcs=[src], dsts=[out for c in to]) for src, out, to, mask, sem in parts],
             local_sem=T.sem["ls"])
         for src, out, to, mask, sem in parts:
-            total["ls"] = total.get("ls", 0) + bits(mask)
-            total[sem] = total.get(sem, 0) + len(to) * bits(mask)
+            comes("ls", bits(mask))
 
-    def spread(src, out, sem):
-        send((src, out, off, common, sem), (src, out, [other], local, sem))
+    if rank is None:
+        boss = served[0]
+        k, e = 4 * T.rank_of(boss), slot(boss)
+        to = far + mates if core == helpers(boss)[0] else plane
+        for t in range(R):
+            num, pln = T["num%d" % t][:, k:k + 1], T["wis%d" % t][:, e:e + E]
+            comes("id%d" % t, wide)
+            wait("g", "id%d" % t)
+            send((num, num, to, common, "id%d" % t))
+            comes("nb%d" % t, wide)
+            wait("g", "nb%d" % t)
+            send((pln, pln, to, common, "nb%d" % t))
+        rest()
+        return
 
-    up(Y.dma_start(T.xt[:, 0:4 * A], T.x[:]), "ldx", 16)
+    other, aides = partner(core), helpers(core)
+    local = topo.mask(core, other) & ~common
+    lower = rank < T.rank_of(other)
+    x0 = NQ - A if lower else 0
+    q0 = A if lower else 2 * A
+    own = q0 + x0
+
+    up(Y.dma_start(T.xt[:, 4 * x0:4 * x0 + 4 * A], T.x[:]), "ldx", 16)
     up(Y.dma_start(T.met[:], T.me[:]), "ldm", 16)
     up(Y.dma_start(T.wt[:], T.w[:]), "ldw", 16)
 
-    up(V.memset(T.xt[:, 4 * A:512], 0.0), "ixt")
+    up(V.memset(T.xt[:, 0:4 * x0] if lower else T.xt[:, 4 * A:512], 0.0), "ixt")
     up(V.memset(T.half[:], 0.5), "ihf")
     up(g.iota(T.ip[:, 0:1], [[1, 1]], 0, 1), "gip")
     up(g.iota(T.c16[:], [[16, 16]], 0, 0, allow_small_or_imprecise_dtypes=True), "gip")
     wait("g", "ihf")
     up(g.affine_select(T.diag[:], T.half[:], [[-1, 128]], OP.is_equal, 0.0, 0, 1), "gdi")
+    up(V.memset(T.et[:], 0.0), "vcc")
     wait("v", "gip")
     up(V.tensor_scalar(T.ia[:, 0:1], T.ip[:, 0:1], 15, None, OP.bitwise_and), "vid")
-    up(V.tensor_copy(T.cst[:, 0:1], T.ip[:, 0:1]), "vp")
+    up(V.memset(T.zz[:], 0.0), "vco")
+    up(V.memset(T.one[:], 1.0), "vco")
     wait("v", "vid")
     up(V.tensor_copy(T.cst[:, 1:2], T.ia[:, 0:1]), "vid")
-    up(V.memset(T.ohb[:], 0.0), "vco")
-    wait("v", "vid")
-    up(V.tensor_scalar(T.cp[:], T.c16[:], T.cst[:, 1:2], None, OP.add), "vid")
-    up(V.memset(T.slb[:], 1.0), "vco")
-    wait("v", "vid")
-    up(V.tensor_copy(T.idl[:], T.cp[:]), "vid")
-    up(V.memset(T.zz[:], 0.0), "vco")
 
     wait("v", "ldx", "ixt")
-    up(V.quantize_mx(T.xq[:], T.xs[:], T.xt[:]), "xqd")
+    up(V.quantize_mx(T.xq[:, q0:q0 + NQ], T.xs[:, q0:q0 + NQ], T.xt[:]), "xqd")
     a = A * rank
     wait("g", "xqd")
-    send((u8("xq", 0, A), lambda c: u8("qa0", a, a + A), off, common, "qx"))
-    spread(T.xs[:, 0:A], lambda c: T.qz0[:, a:a + A], "qx")
-    send((u8("xq", 0, A), lambda c: u8("qa0", a, a + A), [other], local, "qx"))
-    up(g.iota(T.im[:], [[0, 8], [1, 16]], 0, 0, allow_small_or_imprecise_dtypes=True), "gi2")
-    up(g.iota(T.kf[:], [[1, 32]], 0, 0, allow_small_or_imprecise_dtypes=True), "gi2")
-    up(g.iota(T.rst[:], [[0, 256]], 0, 0, allow_small_or_imprecise_dtypes=True), "gi2")
-    wait("g", "gip", "gdi", "gi2")
+    xc, xp = u8("xq", own, own + A), T.xs[:, own:own + A]
+    there = A if lower else NQ + A
+    send((xp, T.xs[:, there:there + A], [other], common, "px"))
+    send((xc, u8("qa0", a, a + A), off, common, "qx"))
+    send((xc, u8("qa0", a, a + A), [other], local, "qx"))
+    send((xp, T.qz0[:, a:a + A], [other], local, "qx"))
+    comes("px", wide)
+    comes("qx", (len(off) + 2 + len(same)) * wide)
+    up(g.iota(T.im[:], [[0, 8], [1, 16]], 0, 0, allow_small_or_imprecise_dtypes=True), "gi1")
+    b = min(a, A * T.rank_of(other))
+    both = own if lower else own - A
+    wait("g", "px")
+    send((T.xs[:, both:both + 2 * A], T.qz0[:, b:b + 2 * A], same, common, "qx"))
+    up(g.iota(T.jr[:], [[-NB, R], [1, NQ]], NB * (R - 1), 0, allow_small_or_imprecise_dtypes=True), "gi2")
+    up(g.iota(T.pl[:], [[int(FAR), M]], 0, 0, allow_small_or_imprecise_dtypes=True), "gi2")
+    wait("g", "gip", "gdi", "gi1", "gi2")
 
-    wait("s", "vp", "vid")
-    up(S.activation(T.cst[:, 8:9], T.cst[:, 0:1], AF.Identity, bias=OUT), "sco")
-    up(S.activation(T.cst[:, 9:10], T.cst[:, 1:2], AF.Identity, bias=0.5), "sco")
-    up(S.activation(T.cst[:, 10:11], T.cst[:, 1:2], AF.Identity, bias=16.5), "sco")
-    for i, p in enumerate(HALVES):
-        up(S.activation(T.cn[p:p + 64, :], T.cp[p:p + 64, 8 * i:8 * i + 8], AF.Copy, scale=-FAR), "sco")
-    wait("s", "xqd")
-    up(S.activation(T.qz0[:, a:a + A], T.xs[:, 0:NQ].indirect(T.idl[:, 0:1]), AF.Copy), "oq")
-    for r in range(N):
-        up(S.activation(T.tab[:, r:r + 1], T.cst[:, 0:1], AF.Identity, bias=float(slot(core, T.cores[r]) - 1),
-                        scale=-1.0), "sco")
-
-    up(V.memset(T.et[:], 0.0), "vcc")
-    wait("v", "vid", "xqd")
-    up(V.tensor_copy(u32("qa0", a, a + A), u32("xq", 0, NQ).indirect(T.idl[:, 0:1])), "oq")
+    wait("v", "vid")
+    up(V.tensor_scalar(T.cp[:], T.c16[:], T.cst[:, 1:2], None, OP.add), "vid")
     wait("v", "vcc", "gdi")
+    up(V.tensor_copy(T.et[:, 3:515:4], T.diag[:]), "vcc")
+    up(V.memset(T.old[:], -FAR), "rs")
+    wait("v", "vid")
+    up(V.tensor_copy(T.idl[:], T.cp[:]), "vid")
+    up(V.memset(T.rst[:], 0.0), "rs")
+
+    wait("s", "vid", "xqd")
+    up(S.activation(T.qz0[:, a:a + A], T.xs[:, own:own + A].indirect(T.idl[:, 0:1]), AF.Copy), "op")
+    for c in range(2):
+        up(S.activation(T.cst[:, 9 + c:10 + c], T.cst[:, 1:2], AF.Identity, bias=-WON * (E - 16 * c), scale=WON), "sco")
+    for i, p in enumerate(HALVES):
+        up(S.activation(T.cn[p:p + 64, 0:8], T.cp[p:p + 64, 8 * i:8 * i + 8], AF.Copy, scale=-FAR), "sco")
+    wait("s", "rs")
+    for i, p in enumerate(HALVES):
+        up(S.activation(T.rst[p:p + 64, 0:256:32], T.cp[p:p + 64, 8 * i:8 * i + 8], AF.Identity, bias=float(R * NB)), "sco")
+    up(S.activation(T.old[:, 0:128:16], T.cp[:, 0:8], AF.Copy), "sco")
+
+    wait("v", "vid", "xqd", "vcc")
+    up(V.tensor_copy(u32("qa0", a, a + A), u32("xq", own, own + A).indirect(T.idl[:, 0:1])), "oq")
     for b in range(4):
-        up(V.tensor_copy(T.et[:, 512 * b + b:512 * b + 512:4], T.diag[:]), "vcc")
+        up(V.quantize_mx(T.eq[:, 128 * b:128 * b + 128], T.ez[:, 128 * b:128 * b + 128], T.et[:, 3 - b:515 - b]), "eqd")
     wait("v", "ldm")
     up(V.quantize_mx(T.mq0[:], T.mz0[:], T.met[:]), "mq0")
-    wait("v", "vcc")
-    up(V.quantize_mx(T.eq[:], T.ez[:], T.et[:]), "eqd")
-    up(V.quantize_mx(T.mw0[:, E:E + M], T.mx0[:, E:E + M], T.met[:]), "mc0")
     for t in range(R):
+        for name, n, m, value in (("wn", 0, 48, WON), ("oh", 0, 48, 0.0), ("sl", 0, 1, 0.0), ("sl", N + 1, N + 2, FAR),
+                                  ("sl", N + 2, N + 3, 1.0), ("sl", N + 3, N + 4, -1.0 / FAR),
+                                  ("cb", 32, 33, -E - 0.5), ("cb", 40, 41, (E + 0.5) * FAR)):
+            o = AT[name][1]
+            up(V.memset(T["h%d" % t][:, o + n:o + m], value), "vco")
         up(V.memset(T["ri%d" % t][:, NQ:RI], 1000.0 * FAR), "vco")
         up(V.memset(T["nt%d" % t][:, 512:520], 0.0), "vco")
-    wait("v", "gi2")
+    up(V.memset(T.tb[:, 0:N], -float(E)), "vco")
+    up(V.memset(T.tb[:, N:N + 1], float(NS)), "vco")
+    wait("v", "gi1")
     up(V.tensor_scalar(T.wm[:], T.im[:, 0:32], T.cst[:, 1:2], None, OP.is_equal), "vco")
     up(V.tensor_scalar(T.nwm[:], T.im[:], T.cst[:, 1:2], None, OP.not_equal), "vco")
-    for i, p in enumerate(HALVES):
-        up(V.tensor_scalar(T.rst[p:p + 64, 0:256:32], T.cp[p:p + 64, 8 * i:8 * i + 8], float(E), None, OP.add), "vco")
+    up(V.quantize_mx(T.mw0[:, R * NB:MW], T.mx0[:, R * NB:MW], T.met[:]), "mc0")
     wait("v", "vco", "sco")
-    up(V.tensor_scalar(T.wp[:], T.wm[:], T.cst[:, 8:9], -OUT, OP.mult, OP.add), "vco")
-    wait("s", "sco")
+    up(V.tensor_scalar(T.wp[:], T.wm[:], -2 * FAR, FAR, OP.mult, OP.add), "vco")
+    wait("s", "sco", "vco")
 
     for t in range(R):
         def B(name, u=t):
@@ -209,239 +256,249 @@ def rank_program(g, core, T, topo):
         def s(name, u=t):
             return "%s%d" % (name, u)
 
+        def h(name, a=0, b=None, step=1, p=0, n=32, u=t):
+            buf, o, w = AT[name]
+            return B(buf, u)[p:p + n, o + a:o + (w if b is None else b):step]
+
         def f(name, a=0, b=None, step=1, u=t):
-            o, w = AT[name]
-            return T["f%d" % u][:, o + a:o + (w if b is None else b):step]
+            return h(name, a, b, step, 0, 128, u)
 
-        def h(name, a=0, b=None, step=1, p=0, n=32):
-            o, w = AT[name]
-            return B("f")[p:p + n, o + a:o + (w if b is None else b):step]
-
-        def sl(a, b):
-            return T.slb[:, 16 * t + a:16 * t + b]
-
-        def oh(u=t):
-            return T.ohb[:, 32 * u:32 * u + 8]
-
-        def fold(row, block, sem):
+        def lanes(out, y, more, sem):
             for p in QUARTERS:
-                up(V.transpose(row[0:32, p:p + 32], block[p:p + 32, :]), sem)
-
-        def lanes(out, y, sem):
-            for p in QUARTERS:
-                up(V.tensor_copy(out[p:p + 32, 0:8], h(y, 15, 128, 16)), sem)
-
-        def whole_of(name, rows=slice(0, 128)):
-            o, w = AT[name]
-            return lambda r, c: B("f")[r, o + c.start:o + c.stop]
+                up(V.tensor_scalar(out[p:p + 32, 0:8], h(y, 15, 128, 16), more, None, OP.add), sem)
 
         def number(step, u=t):
-            where = T.land1[:, 1:32:4] if u == 0 else T.lidx[:, 0:32:4]
             one, vw = (0, 1, 1, u), s("vw", u)
             wait("v", vw)
             if step == 0:
-                up(V.tensor_tensor(f("ol", 0, 8, 1, u), oh(u), where, OP.mult), vw)
+                up(V.tensor_scalar(f("b2", *one), f("kk", 7, 8, 1, u), E + 0.5, 0.5, OP.is_lt, OP.subtract), vw)
+                wait("v", s("id", u), s("ni", u))
+                up(V.tensor_tensor(f("ol", 0, 8, 1, u), f("oh", 0, 8, 1, u), B("num", u)[:, 0:32:4], OP.mult), vw)
             elif step == 1:
                 up(V.tensor_reduce(f("ix", *one), f("ol", 0, 8, 1, u), AX, OP.add), vw)
             else:
                 up(V.tensor_scalar(B("wv", u)[:, 0:1], f("ix", *one), f("b2", *one), -0.5, OP.mult, OP.add), s("wi", u))
 
-        def turn(row, block, sem):
+        def turn(row, block, sem, a=0):
             for p in QUARTERS:
-                up(V.transpose(h(row, p, p + 32), h(block, p=p)), sem)
+                up(V.transpose(h(row, p, p + 32), h(block, a, a + 32, p=p)), sem)
+
+        def pack(u, v, sem):
+            n0 = NB * (R - 1 - u)
+            up(V.quantize_mx(B("mw", v)[:, n0:n0 + 130], B("mx", v)[:, n0:n0 + 130], B("nt", u)[:]), sem)
+
+        def filler(i):
+            if t:
+                number(i, 0)
+            elif i < 2:
+                c = R * NB + H * i
+                up(V.quantize_mx(T.mw1[:, c:c + H], T.mx1[:, c:c + H], T.met[:, 4 * H * i:4 * H * i + 4 * H]), "mc1")
+            else:
+                wait("v", "ldw")
+                up(V.quantize_mx(T.wq[:], T.wz[:], T.wt[:]), "wqd")
 
         one = (0, 1)
-        va, vu, vb, vk, vc, vm = s("va"), s("vu"), s("vb"), s("vk"), s("vc"), s("vm")
+        va, vb, vk, vc, vm, vr = s("va"), s("vb"), s("vk"), s("vc"), s("vm"), s("vr")
         mq, mz, qa, qz = B("mq"), B("mz"), B("qa"), B("qz")
         if t == 0:
-            wait("t", "mq0", "oq", "qx")
+            wait("t", "mq0", "oq", "op", "qx")
         else:
-            wait("t", s("mp", 0), s("rn", 0), s("qp", 0))
-        up(P.matmul_mx(T.psc[:, 0:M], qa[:], qz[:], mq[:], mz[:], True, True), s("sc"))
+            wait("t", s("mp", 0), s("mo", 0), s("rn", 0), s("qp", 0))
+        up(P.matmul_mx(T.psc[:, 0:H], qa[:], qz[:], mq[:, 0:H], mz[:, 0:H], True, True), s("sa"))
+        if t:
+            wait("t", s("m2", 0))
+        up(P.matmul_mx(T.psc[:, 512:512 + H], qa[:], qz[:], mq[:, H:M], mz[:, H:M], True, True), s("sb"))
         wait("t", "eqd")
         if t:
             wait("t", s("nt", 0))
         for b in (0, 1, 2, 3):
             P.matmul_mx(T.pbl[:, 512 * b:512 * b + NQ], T.eq[:, 128 * b:128 * b + 128], T.ez[:, 128 * b:128 * b + 128],
                         qa[:], qz[:], True, False)
-        run, land, k = B("run"), B("land"), 4 * rank
-        wait("v", s("sc"))
-        up(V.tensor_tensor_scan(run[:, 0:M], T.psc[:, 0:M], T.zz[:], LOW, OP.max, OP.add), s("rn"))
+        run, land, num, k = B("run"), B("land"), B("num"), 4 * rank
+        top = run[:, M - 1:M]
+        wait("v", s("sa"))
+        up(V.tensor_tensor_scan(run[:, 0:H], T.psc[:, 0:H], T.zz[:], LOW, OP.max, OP.add), s("ra"))
+        wait("v", s("sb"), s("ra"))
+        up(V.tensor_tensor_scan(run[:, H:M], T.psc[:, 512:512 + H], T.zz[:], run[:, H - 1:H], OP.max, OP.add), s("rn"))
         wait("g", s("rn"))
-        if t == 0:
-            spread(run[:, M - 1:M], lambda c: land[:, k:k + 1], s("ar"))
-        else:
-            wait("g", "orn")
-            spread(run[:, M - 1:M + 1], lambda c: land[:, k:k + 2], s("ar"))
+        send((top, land[:, k:k + 1], off, common, s("ar")), (top, land[:, k:k + 1], [other], local, s("ar")))
+        comes(s("ar"), (N - 1) * wide)
         wait("s", s("rn"))
-        up(S.activation(f("sg"), run[:, 0:M], AF.Sign, bias=run[:, M - 1:M], scale=-1.0, accum_out=f("ti", *one)), s("ix"))
-        up(S.activation(land[:, k:k + 1], run[:, M - 1:M], AF.Copy), s("ow"))
+        up(S.activation(f("sg"), run[:, 0:M], AF.Sign, bias=top, scale=-1.0, accum_out=f("ti", *one)), s("ix"))
+        up(S.activation(land[:, k:k + 1], top, AF.Copy), s("ow"))
         wait("s", s("ix"))
-        base = M * rank + 0.5
-        if t == 0:
-            up(S.activation(T.run1[:, M:M + 1], f("ti", *one), AF.Identity, bias=base), "orn")
-            up(S.activation(T.land1[:, k + 1:k + 2], f("ti", *one), AF.Identity, bias=base), "orn")
-        else:
-            up(S.activation(T.lidx[:, k:k + 1], f("ti", *one), AF.Identity, bias=base), "oli")
+        up(S.activation(num[:, k:k + 1], f("ti", *one), AF.Identity, bias=2.0 * M * rank + 1.0, scale=2.0), s("ni"))
+        wait("g", s("ni"))
+        send((num[:, k:k + 1], num[:, k:k + 1], aides + [other], local, s("id")))
+        comes(s("id"), (N - 1) * wide)
         if t == 0:
             wait("v", "oq", "qx", "vco")
-            wait("s", "oq", "qx")
-            up(V.tensor_copy(u32("win0", 0, NQ), u32("qa0", 0, NQ).indirect(T.idl[:, 0:8])), s("qc"))
-            up(S.activation(T.wis0[:, 0:NQ], T.qz0[:, 0:NQ].indirect(T.idl[:, 0:8]), AF.Copy), s("qc"))
+            wait("s", "op", "qx")
+            up(V.tensor_copy(u32("win0", NS, NS + NQ), u32("qa0", 0, NQ).indirect(T.idl[:, 0:8])), s("qc"))
+            up(S.activation(T.wis0[:, NS:NS + NQ], T.qz0[:, 0:NQ].indirect(T.idl[:, 0:8]), AF.Copy), s("qc"))
         else:
-            up(V.tensor_copy(u32("win1", 0, NQ), u32("win0", 0, NQ + N * E).indirect(T.offq0[:, 0:8])), s("qc"))
-            up(S.activation(T.wis1[:, 0:NQ], T.wis0[:, 0:NQ + N * E].indirect(T.offq0[:, 0:8]), AF.Copy), s("qc"))
-            wait("g", "oli")
-            spread(T.lidx[:, k:k + 1], lambda c: T.lidx[:, k:k + 1], "idx")
-            wait("y", s("mp", 0), s("ar"))
-            up(Y.dma_start(u8("mw1", E, E + M), u8("mq1", 0, M)), "mc1", 16)
-            up(Y.dma_start(T.mx1[:, E:E + M], T.mz1[:]), "mc1", 16)
+            up(V.tensor_copy(u32("win1", NS, NS + NQ), u32("win0", 0, NS + NQ).indirect(T.offq0[:, 0:8])), s("qc"))
+            up(S.activation(T.wis1[:, NS:NS + NQ], T.wis0[:, 0:NS + NQ].indirect(T.offq0[:, 0:8]), AF.Copy), s("qc"))
+            pack(0, 1, "mc1")
         wait("v", s("ix"))
         up(V.tensor_scalar(f("ra"), T.wm[:], f("ti", *one), None, OP.mult), va)
-        up(V.tensor_scalar(f("ru"), T.zz[:, 0:32], f("ti", *one), FAR, OP.add, OP.mult), vu)
+        filler(0)
         wait("v", va)
         turn("la", "ra", va)
+        filler(1)
         wait("v", va)
         up(V.tensor_tensor_scan(h("ly"), T.nwm[0:32, :], h("la"), 0.0, OP.mult, OP.add), va)
+        filler(2)
         wait("v", va)
-        lanes(B("offi"), "ly", s("oi"))
-        wait("v", s("oi"))
+        lanes(B("offi"), "ly", 0.0, s("oi"))
+        wait("v", s("oi"), "mp0", "m20")
         up(V.tensor_copy(u32(s("pm"), 0, NQ), u32(s("mq"), 0, M).indirect(B("offi")[:, 0:8])), s("pm"))
         wait("s", s("oi"))
         up(S.activation(B("pz")[:, 0:NQ], mz[:, 0:M].indirect(B("offi")[:, 0:8]), AF.Copy), s("pm"))
         ri = B("ri")
-        wait("v", vu)
-        turn("rr", "ru", vu)
-        wait("g", vu)
-        up(g.partition_broadcast(ri[:, 0:NQ], h("rr", n=1), 128), s("rb"))
+
+        def places(i):
+            up(V.tensor_tensor(ri[:, 64 * i:64 * i + 64], T.pl[:, 0:M].indirect(B("offi")[:, 4 * i:4 * i + 4]),
+                               T.jr[:, NQ * t + 64 * i:NQ * t + 64 * i + 64], OP.add), s("rb"))
+
         wait("t", s("pm"))
         bank = {0: s("ba"), 1: s("bb"), 2: s("bc"), 3: s("bd")}
         for b in (0, 1, 2, 3):
             up(P.matmul_mx(T.pbl[:, 512 * b:512 * b + NQ], T.eq[:, 128 * b:128 * b + 128], T.ez[:, 128 * b:128 * b + 128],
                            B("pm")[:], B("pz")[:], False, True), bank[b])
         nt = B("nt")
-        wait("v", bank[0])
-        up(V.tensor_copy(nt[:, 0:512:4], T.pbl[:, 0:NQ]), s("nt"))
-        for b in (1, 2, 3):
+        for b in (0, 1, 2):
             wait("s", bank[b])
             up(S.activation(nt[:, b:512:4], T.pbl[:, 512 * b:512 * b + NQ], AF.Copy), s("nt"))
-        wait("v", s("ow"), s("ar"))
-        up(V.tensor_tensor_scan(f("rl"), land[:, 0:32:4], T.zz[:, 0:8], LOW, OP.max, OP.add), vb)
+        wait("v", "gi2")
+        places(0)
+        wait("v", s("ar"))
+        if rank > 0:
+            up(V.tensor_scalar(f("wn", 0, rank), land[:, 0:k:4], top, WON, OP.is_lt, OP.mult), vb)
+        if rank < N - 1:
+            up(V.tensor_scalar(f("wn", rank + 1, N), land[:, k + 4:32:4], top, WON, OP.is_le, OP.mult), vb)
+        wait("v", s("ow"))
+        up(V.tensor_tensor_scan(f("rl"), land[:, 0:32:4], T.zz[:, 0:8], LOW, OP.max, OP.add), vr)
+        places(1)
         wait("v", vb)
-        up(V.tensor_scalar(sl(1, 9), f("rl"), f("rl", 7, 8), None, OP.is_lt), vb)
+        up(V.tensor_tensor_scan(f("fr", 0, 40), f("wn", 0, 40), f("wn", 0, 40), WON, OP.max, OP.max), vb)
+        wait("v", vr)
+        up(V.tensor_scalar(f("sl", 1, N + 1), f("rl"), f("rl", 7, 8), None, OP.is_ge), vr)
         wait("v", vb)
-        up(V.tensor_scalar(f("fr"), T.zz[:, 0:32], sl(rank, rank + 1), sl(rank + 1, rank + 2), OP.add, OP.subtract), vb)
-        up(V.tensor_tensor(oh(), sl(0, 8), sl(1, 9), OP.subtract), vc)
+        turn("ft", "fr", vb, 8)
+        wait("v", vr)
+        up(V.tensor_tensor(f("oh", 0, N), f("sl", 1, N + 1), f("sl", 0, N), OP.subtract), vc)
+        up(V.tensor_tensor_scan(f("cb", 12, 37, 3), T.tb[:, 0:N + 1], f("sl", 1, N + 2), 0.0, OP.add, OP.mult), vr)
         wait("v", vb)
-        turn("ft", "fr", vb)
+        up(V.tensor_tensor_scan(h("sa"), h("ft"), T.one[0:32, :], T.cst[0:32, 9:10], OP.add, OP.add), vb)
+        up(V.tensor_tensor_scan(h("sb"), h("ft"), T.one[0:32, :], T.cst[0:32, 10:11], OP.add, OP.add), s("ac"))
+        wait("v", bank[3])
+        up(V.tensor_copy(nt[:, 3:512:4], T.pbl[:, 1536:1536 + NQ]), s("nt"))
         wait("v", vb)
-        up(V.tensor_tensor_scan(h("cn"), h("ft"), T.zz[0:32, 0:128], 0.0, OP.add, OP.add), vb)
-        wait("s", vb)
-        up(S.activation(h("sa"), h("cn"), AF.Sign, bias=T.cst[0:32, 9:10], scale=-1.0, accum_out=h("acc", 0, 1)), s("ac"))
-        up(S.activation(h("sb"), h("cn"), AF.Sign, bias=T.cst[0:32, 10:11], scale=-1.0, accum_out=h("acc", 1, 2)), s("ac"))
-        wait("v", vc)
-        for p in QUARTERS:
-            up(V.transpose(h("ot", p, p + 32), T.ohb[p:p + 32, 32 * t:32 * t + 32]), vc)
-        wait("v", s("nt"))
-        up(V.quantize_mx(B("nq")[:, 0:130], B("nz")[:, 0:130], nt[:]), s("nq"))
+        up(V.tensor_reduce(h("acc", 0, 1), h("sa"), AX, OP.min, apply_absolute_value=True), vb)
         wait("v", s("ac"))
-        offs = B("offs")
+        up(V.tensor_reduce(h("acc", 1, 2), h("sb"), AX, OP.min, apply_absolute_value=True), vb)
+        wait("v", s("nt"))
+        pack(t, t, s("nq"))
+        wait("v", vb)
+        offs, n0, e = B("offs"), NB * (R - 1 - t), slot(core)
         for p in QUARTERS:
-            up(V.tensor_scalar(offs[p:p + 32, 0:2], h("acc", 0, 2), 0.5, 64.0, OP.mult, OP.add), s("os"))
+            up(V.tensor_scalar(offs[p:p + 32, 0:2], h("acc", 0, 2), NQ + 1.0, -1.0, OP.min, OP.add), s("os"))
+        wait("v", vc)
+        up(V.tensor_tensor(f("dd", 0, 32, 4), f("oh", 0, N), f("oh", 1, N + 1), OP.subtract), vc)
         wait("v", s("os"), s("nq"))
-        up(V.tensor_copy(u32(s("mw"), 0, E), u32(s("nq"), 0, 130).indirect(offs[:, 0:2])), s("sl"))
+        up(V.tensor_copy(u32(s("win"), e, e + E), u32(s("mw"), n0, n0 + 130).indirect(offs[:, 0:2])), s("sl"))
         wait("s", s("nq"), s("os"))
-        up(S.activation(B("mx")[:, 0:E], B("nz")[:, 0:130].indirect(offs[:, 0:2]), AF.Copy), s("sz"))
-
-        def codes(c):
-            return u8(s("win"), slot(c, core), slot(c, core) + E)
-
-        wait("g", s("sl"))
-        send((u8(s("mw"), 0, E), codes, same, common, s("na")), (u8(s("mw"), 0, E), codes, [other], local, s("nx")))
+        up(S.activation(B("wis")[:, e:e + E], B("mx")[:, n0:n0 + 130].indirect(offs[:, 0:2]), AF.Copy), s("sz"))
+        codes, planes = u8(s("win"), e, e + E), B("wis")[:, e:e + E]
         wait("g", s("sz"))
-        spread(B("mx")[:, 0:E], lambda c: B("wis")[:, slot(c, core):slot(c, core) + E], s("nb"))
+        send((planes, planes, aides[:1], common, s("nb")), (planes, planes, aides[1:] + [other], local, s("nb")))
+        wait("g", s("sl"))
+        send((codes, codes, far[:1], common, s("na")), (codes, codes, [other], local, s("nx")))
+        send((codes, codes, plane + mates, common, s("nx")))
+        comes(s("na"), wide)
+        comes(s("nb"), (N - 1) * wide)
+        comes(s("nx"), (N - 2) * wide)
         wait("g", s("na"))
-        n = E * len(same)
-        send((u8(s("win"), NQ, NQ + n), lambda c: u8(s("win"), NQ + n, NQ + 2 * n), [other], whole, s("nx")))
-        e = slot(core, core)
-        wait("v", s("rb"))
-        up(V.tensor_tensor(B("uu")[:, 0:E], ri[:, 0:RI].indirect(offs[:, 0:2]), T.kf[:], OP.add), s("u1"))
-        wait("s", s("u1"))
+        came = u8(s("win"), slot(far[0]), slot(far[0]) + E)
+        send((came, came, [other], local, s("nx")))
+        wait("s", s("rb"))
         for c in range(8):
-            up(S.activation(f("ab", 32 * c, 32 * c + 32), B("uu")[:, 0:E], AF.Abs, bias=T.cn[:, c:c + 1], scale=1.0),
-               s("ab"))
-        up(S.activation(B("wis")[:, e:e + E], B("nz")[:, 0:130].indirect(offs[:, 0:2]), AF.Copy), s("oz"))
+            up(S.activation(f("ab", E * c, E * c + E), ri[:, 0:RI].indirect(offs[:, 0:2]), AF.Abs, bias=T.cn[:, c:c + 1],
+                            scale=1.0), s("ab"))
         wait("v", vc)
-        up(V.tensor_tensor_scan(h("ct"), h("ot"), T.zz[0:32, 0:128], 0.0, OP.add, OP.add), vc)
-        up(V.tensor_tensor(f("t0"), T.tab[:], oh(), OP.mult), vk)
-        wait("v", vc)
-        for p in QUARTERS:
-            up(V.transpose(h("cb", p=p), h("ct", p, p + 32)), vc)
+        turn("ot", "dd", vk)
         wait("v", vk)
-        up(V.tensor_reduce(f("t1", *one), f("t0"), AX, OP.add), vk)
+        up(V.tensor_tensor_scan(h("ct"), h("ot"), T.zz[0:32, :], 0.0, OP.add, OP.add), vc)
+        wait("v", vc, vr)
+        for p in QUARTERS:
+            up(V.transpose(h("cb", 0, 32, p=p), h("ct", p, p + 32)), vc)
         wait("v", vc)
-        up(V.tensor_tensor(f("kr"), f("cb", 0, 8), oh(), OP.mult), vc)
-        up(V.tensor_copy(u32(s("win"), e, e + E), u32(s("nq"), 0, 130).indirect(offs[:, 0:2])), s("on"))
-        wait("v", vc)
-        up(V.tensor_reduce(f("kk", *one), f("kr"), AX, OP.add), vc)
-        if t:
-            wait("v", "orn")
-            number(0, 0)
-        wait("v", vc)
-        up(V.tensor_scalar(f("an", *one), f("kk", *one), E + 0.5, None, OP.is_lt), vc)
-        if t:
-            number(1, 0)
-        wait("v", vc, vk)
-        up(V.tensor_scalar(f("tt", *one), f("kk", *one), f("t1", *one), f("an", *one), OP.add, OP.mult), vc)
-        up(V.tensor_scalar(f("b2", *one), f("an", *one), 2.0, -1.0, OP.mult, OP.add), s("vw"))
-        wait("v", vc)
-        up(V.tensor_scalar(f("rc"), T.wp[:], f("tt", *one), 0.0, OP.add, OP.max), vc)
-        if t:
-            number(2, 0)
-        wait("v", vc)
-        turn("lc", "rc", vc)
-        wait("v", vc)
-        up(V.tensor_tensor_scan(h("oy"), T.nwm[0:32, :], h("lc"), 0.0, OP.mult, OP.add), vc)
+        up(V.tensor_tensor_scan(f("kk", 0, 11), f("cb", 0, 44, 4), f("sl", 1, N + 4), 0.0, OP.add, OP.mult), vc)
         wait("v", s("ab"))
         up(V.tensor_tensor_scan(f("am"), T.rst[:], f("ab"), 0.0, OP.max, OP.min), vm)
         wait("v", vc)
-        lanes(B("offq"), "oy", s("od"))
-        wait("v", vm)
-        for p in HALVES:
+        up(V.tensor_scalar(f("rc"), T.wp[:], f("kk", 8, 9), f("kk", 10, 11), OP.max, OP.max), vc)
+
+        def spread(p):
             for i, q in enumerate(HALVES):
                 up(V.tensor_copy(B("offm")[p:p + 64, 8 * i:8 * i + 8], h("am", 31, 256, 32, p=q, n=64)), s("om"))
+
+        wait("v", vm)
         if t:
-            wait("v", "idx", "oli")
+            up(V.tensor_tensor(f("am", 31, 256, 32), f("am", 31, 256, 32), f("am", 31, 256, 32, 0), OP.min), vm)
             number(0, 1)
         else:
-            wait("v", "ldw")
-            up(V.quantize_mx(T.wq[:], T.wz[:], T.wt[:]), "wqd")
-        wait("v", s("om"), s("sl"), s("mc"))
-        mp = s("mp")
-        up(V.tensor_copy(u32(s("mq", t + 1), 0, M), u32(s("mw"), 0, M + E).indirect(B("offm")[:, 0:16])), mp)
-        wait("s", s("om"), s("sz"), s("mc"))
-        up(S.activation(B("mz", t + 1)[:, 0:M], B("mx")[:, 0:M + E].indirect(B("offm")[:, 0:16]), AF.Copy), mp)
+            spread(0)
+            spread(64)
+        wait("v", vc)
+        turn("lc", "rc", vc)
         if t:
+            wait("v", vm)
+            spread(0)
+        else:
+            wait("v", s("om"), s("mc"))
+            up(V.tensor_copy(u32(s("mq", t + 1), 0, H), u32(s("mw"), 0, MW).indirect(B("offm")[:, 0:8])), s("mp"))
+        wait("v", vc)
+        up(V.tensor_tensor_scan(h("oy"), T.old[0:32, :], h("lc"), -FAR, OP.max, OP.min), vc)
+        if t:
+            spread(64)
             number(1, 1)
+        wait("v", vc)
+        lanes(B("offq"), "oy", float(NS), s("od"))
+        if t:
             number(2, 1)
-        wait("v", s("od"), s("on"), s("qc"), s("na"), s("nx"))
-        wait("s", s("od"), s("oz"), s("qc"), s("nb"))
-        up(V.tensor_copy(u32(s("qa", t + 1), 0, NQ), u32(s("win"), 0, NQ + N * E).indirect(B("offq")[:, 0:8])), s("qp"))
-        up(S.activation(B("qz", t + 1)[:, 0:NQ], B("wis")[:, 0:NQ + N * E].indirect(B("offq")[:, 0:8]), AF.Copy), s("qp"))
+        wait("s", s("om"), s("mc"))
+        for i in range(2):
+            up(S.activation(B("mz", t + 1)[:, H * i:H * i + H], B("mx")[:, 0:MW].indirect(B("offm")[:, 8 * i:8 * i + 8]),
+                            AF.Copy), s("mo"))
+            if t and i == 0:
+                wait("s", s("od"), s("sz"), s("qc"), s("nb"))
+                up(S.activation(T.qz2[:, 0:NQ], B("wis")[:, 0:NS + NQ].indirect(B("offq")[:, 0:8]), AF.Copy), s("qp"))
+        wait("v", s("od"), s("sl"), s("qc"), s("na"), s("nx"))
+        up(V.tensor_copy(u32(s("qa", t + 1), 0, NQ), u32(s("win"), 0, NS + NQ).indirect(B("offq")[:, 0:8])), s("qp"))
+        if t:
+            wait("v", s("om"), s("mc"))
+            up(V.tensor_copy(u32(s("mq", t + 1), 0, H), u32(s("mw"), 0, MW).indirect(B("offm")[:, 0:8])), s("mp"))
+        else:
+            wait("s", s("od"), s("sz"), s("qc"), s("nb"))
+            up(S.activation(T.qz1[:, 0:NQ], B("wis")[:, 0:NS + NQ].indirect(B("offq")[:, 0:8]), AF.Copy), s("qp"))
+        up(V.tensor_copy(u32(s("mq", t + 1), H, M), u32(s("mw"), 0, MW).indirect(B("offm")[:, 8:16])), s("m2"))
 
-    wait("y", "mp1", "nx1", "nb1")
-    up(Y.dma_start(T.oc[:, 0:4 * M], u8("mq%d" % R, 0, M)), "st", 16)
-    for c in range(4):
-        up(Y.dma_start(T.osc[4 * c:4 * c + 4, 0:M], T["mz%d" % R][32 * c:32 * c + 4, 0:M]), "st", 16)
     wait("y", "wi0", "wi1")
     for u in range(R):
         up(Y.dma_start(T.wi[u:u + 1, :], T["wv%d" % u][:, 0:1]), "st", 16)
+    wait("y", "mp1")
+    up(Y.dma_start(T.oc[:, 0:4 * H], u8("mq%d" % R, 0, H)), "st", 16)
+    wait("y", "mo1")
+    for c in range(4):
+        up(Y.dma_start(T.osc[4 * c:4 * c + 4, 0:M], T["mz%d" % R][32 * c:32 * c + 4, 0:M]), "st", 16)
+    wait("y", "m21")
+    up(Y.dma_start(T.oc[:, 4 * H:4 * M], u8("mq%d" % R, H, M)), "st", 16)
     wait("t", "wqd", "qp1")
     up(P.matmul_mx(T.pyy[:, 0:NQ], T.wq[:], T.wz[:], T.qa2[:], T.qz2[:], True, True), "yp")
     wait("v", "yp")
     up(V.tensor_copy(T.yt[:], T.pyy[:, 0:NQ]), "yc")
     wait("s", "yc")
     up(S.dma_start(T.y[:], T.yt[:]), "sty", 16)
-    for name in total:
-        if seen.get(("", name), 0) < total[name]:
-            wait("g", name)
+    rest()

@@ -10,15 +10,18 @@ AF = ActivationFunctionType
 AX = AxisListType.X
 LOW = -9.0e29
 FAR = 1024.0
-WON = -256.0
-NB = 160
-MW = R * NB + M
+WON = 256.0
+STEP = 1.25 * 2.0 ** -24
+TINY = 1.0e-37
+MW = M + R * E
+EK = E + 1
 RI = NQ + 8
 
-WORK = [("ti", 8), ("acc", 8), ("rl", 8), ("kk", 16), ("ol", 8), ("ix", 8), ("b2", 8),
-        ("sg", 256), ("ab", 256), ("am", 256)]
-HALF = [("ra", 32), ("la", 128), ("ly", 128), ("wn", 48), ("fr", 48), ("ft", 128), ("sa", 128), ("sb", 128),
-        ("oh", 16), ("dd", 32), ("ot", 128), ("ct", 128), ("cb", 48), ("sl", 16), ("rc", 32), ("lc", 128), ("oy", 128)]
+WORK = [("ti", 8), ("eps", 8), ("thr", 8), ("rl", 8), ("kk", 16), ("ol", 8), ("ix", 8), ("b2", 8),
+        ("sg", 256), ("ab", 8 * EK), ("am", 8 * EK)]
+HALF = [("wn", 48), ("oh", 16), ("dd", 32), ("cb", 48), ("sl", 16),
+        ("ra", 32), ("la", 128), ("ly", 128), ("fr", 48), ("ft", 128), ("sa", 128), ("sb", 128), ("sc", 256),
+        ("ot", 128), ("ct", 128), ("rc", 32), ("lc", 128), ("oy", 128)]
 AT = {}
 _n = {}
 for _b, _l in (("f", WORK), ("h", HALF)):
@@ -26,6 +29,7 @@ for _b, _l in (("f", WORK), ("h", HALF)):
     for _name, _w in _l:
         AT[_name] = (_b, _n[_b], _w)
         _n[_b] += _w
+PRE = AT["ra"][1]
 
 SCRATCH = {
     "xt": ("sbuf", [128, 512], "bfloat16"), "met": ("sbuf", [128, 4 * M], "bfloat16"),
@@ -34,16 +38,16 @@ SCRATCH = {
     "xq": ("sbuf", [128, 160], "float8_e4m3fn_x4"), "xs": ("sbuf", [128, 160], "uint8"),
     "wq": ("sbuf", [128, 128], "float8_e4m3fn_x4"), "wz": ("sbuf", [128, 128], "uint8"),
     "eq": ("sbuf", [128, 512], "float8_e4m3fn_x4"), "ez": ("sbuf", [128, 512], "uint8"),
-    "zz": ("sbuf", [128, 128], "bfloat16"), "one": ("sbuf", [128, 128], "bfloat16"),
-    "wm": ("sbuf", [128, 32], "bfloat16"), "nwm": ("sbuf", [128, 128], "bfloat16"),
+    "zz": ("sbuf", [128, M], "bfloat16"), "down": ("sbuf", [128, 128], "bfloat16"), "dn": ("sbuf", [128, 48], "bfloat16"),
+    "wm": ("sbuf", [128, 32], "bfloat16"), "nwm": ("sbuf", [128, 128], "bfloat16"), "ini": ("sbuf", [128, 8], "bfloat16"),
     "wp": ("sbuf", [128, 32], "bfloat16"), "old": ("sbuf", [128, 128], "bfloat16"), "tb": ("sbuf", [128, 16], "float32"),
-    "rst": ("sbuf", [128, 256], "float32"), "im": ("sbuf", [128, 128], "float32"), "pl": ("sbuf", [128, M], "float32"),
-    "ip": ("sbuf", [128, 8], "int32"), "ia": ("sbuf", [128, 8], "int32"), "jr": ("sbuf", [128, R * NQ], "float32"),
+    "rst": ("sbuf", [128, 8 * EK], "float32"), "im": ("sbuf", [128, 128], "float32"), "pl": ("sbuf", [128, M], "float32"),
+    "ip": ("sbuf", [128, 8], "int32"), "ia": ("sbuf", [128, 8], "int32"),
     "c16": ("sbuf", [128, 16], "float32"), "cp": ("sbuf", [128, 16], "float32"),
     "cn": ("sbuf", [128, 8], "float32"),
-    "cst": ("sbuf", [128, 32], "float32"), "yt": ("sbuf", [128, 128], "float32"),
+    "cst": ("sbuf", [128, 8], "float32"), "yt": ("sbuf", [128, 128], "float32"),
     "idl": ("sbuf", [128, 16], "uint16"),
-    "psc": ("psum", [128, 1024], "float32"), "pbl": ("psum", [128, 2048], "float32"), "pyy": ("psum", [128, 512], "float32"),
+    "psc": ("psum", [128, 512], "float32"), "pbl": ("psum", [128, 2048], "float32"), "pyy": ("psum", [128, 512], "float32"),
 }
 for _t in range(R + 1):
     SCRATCH["mq%d" % _t] = ("sbuf", [128, M], "float8_e4m3fn_x4")
@@ -54,16 +58,17 @@ for _t in range(R):
     for _name, _w, _d in (("mw", MW, "float8_e4m3fn_x4"), ("mx", MW, "uint8"),
                           ("win", NS + NQ, "float8_e4m3fn_x4"), ("wis", NS + NQ, "uint8"),
                           ("pm", NQ, "float8_e4m3fn_x4"), ("pz", NQ, "uint8"),
+                          ("nq", 160, "float8_e4m3fn_x4"), ("nz", 160, "uint8"),
                           ("nt", 520, "bfloat16"), ("run", M, "float32"), ("land", 32, "float32"), ("num", 32, "float32"),
                           ("ri", RI, "float32"), ("wv", 8, "float32"),
                           ("f", _n["f"], "float32"), ("h", _n["h"], "bfloat16"),
                           ("offi", 8, "uint16"), ("offs", 2, "uint16"), ("offm", 16, "uint16"), ("offq", 8, "uint16")):
         SCRATCH["%s%d" % (_name, _t)] = ("sbuf", [128, _w], _d)
 
-ONCE = ["ldx", "ldm", "ldw", "ixt", "ihf", "gdi", "gip", "gi1", "gi2", "xqd", "eqd", "wqd", "qx", "px", "oq", "op", "mq0",
-        "vcc", "vco", "vid", "ls", "yp", "yc", "st", "sty", "sco", "rs"]
-EACH = ["sa", "sb", "ra", "rn", "ix", "ow", "oi", "pm", "ba", "bb", "bc", "bd", "nt", "nq", "ar", "ac", "os", "sl", "sz",
-        "ab", "om", "mp", "mo", "od", "nx", "qp", "qc", "wi", "va", "vb", "vk", "vc", "vm", "vw", "na",
+ONCE = ["ldx", "ldm", "ldw", "ixt", "ihf", "gdi", "gip", "gi1", "gi2", "gi3", "xqd", "eqd", "wqd", "qx", "px", "vz", "oq",
+        "op", "mq0", "vcc", "vco", "vid", "ls", "yp", "yc", "st", "sty", "sco", "rs", "pre"]
+EACH = ["sa", "rn", "ix", "ow", "oi", "pm", "ba", "bb", "bc", "bd", "nt", "nq", "ar", "ac", "os", "sl",
+        "sz", "ab", "om", "mp", "mo", "od", "nx", "qp", "qc", "wi", "va", "vb", "vk", "vc", "vm", "vw",
         "nb", "rb", "ni", "id", "vr", "m2", "mc"]
 SEMAPHORES = ONCE + ["%s%d" % (_s, _t) for _s in EACH for _t in range(R)]
 QUARTERS = (0, 32, 64, 96)
@@ -125,7 +130,8 @@ def rank_program(g, core, T, topo):
         return (2 if topo.mates(here, k) else 1 if topo.same_plane(here, k) else 0, topo.die(c) != topo.die(core))
 
     off = sorted([c for c in T.cores if topo.chip(c) != here], key=near)
-    far, plane, mates = [[c for c in off if near(c)[0] == i] for i in range(3)]
+    plane = [c for c in off if near(c)[0] == 1]
+    across = [c for c in off if c not in plane]
     same = [c for c in off if topo.die(c) == topo.die(core)]
     common = topo.mask(core, off[0])
     for c in off:
@@ -147,15 +153,16 @@ def rank_program(g, core, T, topo):
     if rank is None:
         boss = served[0]
         k, e = 4 * T.rank_of(boss), slot(boss)
-        to = far + mates if core == helpers(boss)[0] else plane
+        to = across if core == helpers(boss)[0] else plane
+        c = min(e, slot(partner(boss)))
         for t in range(R):
-            num, pln = T["num%d" % t][:, k:k + 1], T["wis%d" % t][:, e:e + E]
+            num, pln = T["num%d" % t][:, k:k + 1], T["wis%d" % t][:, c:c + 2 * E]
             comes("id%d" % t, wide)
             wait("g", "id%d" % t)
             send((num, num, to, common, "id%d" % t))
-            comes("nb%d" % t, wide)
+            comes("nb%d" % t, 2 * wide)
             wait("g", "nb%d" % t)
-            send((pln, pln, to, common, "nb%d" % t))
+            send((pln, pln, [d for d in to if d in same], common, "nb%d" % t))
         rest()
         return
 
@@ -176,11 +183,10 @@ def rank_program(g, core, T, topo):
     up(g.iota(T.c16[:], [[16, 16]], 0, 0, allow_small_or_imprecise_dtypes=True), "gip")
     wait("g", "ihf")
     up(g.affine_select(T.diag[:], T.half[:], [[-1, 128]], OP.is_equal, 0.0, 0, 1), "gdi")
-    up(V.memset(T.et[:], 0.0), "vcc")
+    up(V.memset(T.zz[:], 0.0), "vz")
     wait("v", "gip")
     up(V.tensor_scalar(T.ia[:, 0:1], T.ip[:, 0:1], 15, None, OP.bitwise_and), "vid")
-    up(V.memset(T.zz[:], 0.0), "vco")
-    up(V.memset(T.one[:], 1.0), "vco")
+    up(V.memset(T.h0[:, 0:PRE], 0.0), "vz")
     wait("v", "vid")
     up(V.tensor_copy(T.cst[:, 1:2], T.ia[:, 0:1]), "vid")
 
@@ -196,58 +202,60 @@ def rank_program(g, core, T, topo):
     send((xp, T.qz0[:, a:a + A], [other], local, "qx"))
     comes("px", wide)
     comes("qx", (len(off) + 2 + len(same)) * wide)
-    up(g.iota(T.im[:], [[0, 8], [1, 16]], 0, 0, allow_small_or_imprecise_dtypes=True), "gi1")
     b = min(a, A * T.rank_of(other))
     both = own if lower else own - A
     wait("g", "px")
     send((T.xs[:, both:both + 2 * A], T.qz0[:, b:b + 2 * A], same, common, "qx"))
-    up(g.iota(T.jr[:], [[-NB, R], [1, NQ]], NB * (R - 1), 0, allow_small_or_imprecise_dtypes=True), "gi2")
-    up(g.iota(T.pl[:], [[int(FAR), M]], 0, 0, allow_small_or_imprecise_dtypes=True), "gi2")
-    wait("g", "gip", "gdi", "gi1", "gi2")
+    up(g.iota(T.im[:], [[0, 8], [1, 16]], 0, 0, allow_small_or_imprecise_dtypes=True), "gi1")
+    up(g.iota(T.down[0:32, :], [[-1, NQ]], NQ - 1, 0, allow_small_or_imprecise_dtypes=True), "gi2")
 
-    wait("v", "vid")
+    up(V.memset(T.et[:], 0.0), "vcc")
+    wait("v", "vid", "vz")
     up(V.tensor_scalar(T.cp[:], T.c16[:], T.cst[:, 1:2], None, OP.add), "vid")
+    up(V.memset(T.old[:], -FAR), "rs")
     wait("v", "vcc", "gdi")
     up(V.tensor_copy(T.et[:, 3:515:4], T.diag[:]), "vcc")
-    up(V.memset(T.old[:], -FAR), "rs")
     wait("v", "vid")
     up(V.tensor_copy(T.idl[:], T.cp[:]), "vid")
-    up(V.memset(T.rst[:], 0.0), "rs")
 
-    wait("s", "vid", "xqd")
+    def fill(out, n, value):
+        up(S.activation(out, T.zz[:, 0:n], AF.Identity, bias=value), "sco")
+
+    wait("s", "vz", "vid", "xqd")
     up(S.activation(T.qz0[:, a:a + A], T.xs[:, own:own + A].indirect(T.idl[:, 0:1]), AF.Copy), "op")
     for c in range(2):
-        up(S.activation(T.cst[:, 9 + c:10 + c], T.cst[:, 1:2], AF.Identity, bias=-WON * (E - 16 * c), scale=WON), "sco")
+        up(S.activation(T.ini[:, 2 * c:2 * c + 1], T.cst[:, 1:2], AF.Identity, bias=NQ - WON * (E - 16 * c), scale=WON),
+           "sco")
     for i, p in enumerate(HALVES):
         up(S.activation(T.cn[p:p + 64, 0:8], T.cp[p:p + 64, 8 * i:8 * i + 8], AF.Copy, scale=-FAR), "sco")
     wait("s", "rs")
-    for i, p in enumerate(HALVES):
-        up(S.activation(T.rst[p:p + 64, 0:256:32], T.cp[p:p + 64, 8 * i:8 * i + 8], AF.Identity, bias=float(R * NB)), "sco")
     up(S.activation(T.old[:, 0:128:16], T.cp[:, 0:8], AF.Copy), "sco")
+    fill(T.tb[:, 0:N], N, -float(E))
+    fill(T.tb[:, N:N + 1], 1, float(NS))
 
+    for name, n, m, value in (("wn", 0, 48, WON), ("sl", N + 1, N + 2, FAR), ("sl", N + 2, N + 3, 1.0),
+                              ("sl", N + 3, N + 4, -1.0 / FAR), ("cb", 32, 33, -E - 0.5), ("cb", 40, 41, (E + 0.5) * FAR)):
+        o = AT[name][1]
+        up(V.memset(T.h0[:, o + n:o + m], value), "pre")
     wait("v", "vid", "xqd", "vcc")
     up(V.tensor_copy(u32("qa0", a, a + A), u32("xq", own, own + A).indirect(T.idl[:, 0:1])), "oq")
     for b in range(4):
         up(V.quantize_mx(T.eq[:, 128 * b:128 * b + 128], T.ez[:, 128 * b:128 * b + 128], T.et[:, 3 - b:515 - b]), "eqd")
+    wait("v", "pre")
+    up(V.tensor_copy(T.h1[:, 0:PRE], T.h0[:, 0:PRE]), "vco")
     wait("v", "ldm")
     up(V.quantize_mx(T.mq0[:], T.mz0[:], T.met[:]), "mq0")
+    o = AT["ab"][1]
     for t in range(R):
-        for name, n, m, value in (("wn", 0, 48, WON), ("oh", 0, 48, 0.0), ("sl", 0, 1, 0.0), ("sl", N + 1, N + 2, FAR),
-                                  ("sl", N + 2, N + 3, 1.0), ("sl", N + 3, N + 4, -1.0 / FAR),
-                                  ("cb", 32, 33, -E - 0.5), ("cb", 40, 41, (E + 0.5) * FAR)):
-            o = AT[name][1]
-            up(V.memset(T["h%d" % t][:, o + n:o + m], value), "vco")
         up(V.memset(T["ri%d" % t][:, NQ:RI], 1000.0 * FAR), "vco")
+        up(V.memset(T["f%d" % t][:, o:o + 8 * EK:EK], 0.0), "vco")
         up(V.memset(T["nt%d" % t][:, 512:520], 0.0), "vco")
-    up(V.memset(T.tb[:, 0:N], -float(E)), "vco")
-    up(V.memset(T.tb[:, N:N + 1], float(NS)), "vco")
+    for n, m, value in ((0, N, 1.0), (N, N + 1, WON), (N + 1, 48, 1.0)):
+        up(V.memset(T.dn[:, n:m], value), "vco")
     wait("v", "gi1")
     up(V.tensor_scalar(T.wm[:], T.im[:, 0:32], T.cst[:, 1:2], None, OP.is_equal), "vco")
     up(V.tensor_scalar(T.nwm[:], T.im[:], T.cst[:, 1:2], None, OP.not_equal), "vco")
-    up(V.quantize_mx(T.mw0[:, R * NB:MW], T.mx0[:, R * NB:MW], T.met[:]), "mc0")
-    wait("v", "vco", "sco")
-    up(V.tensor_scalar(T.wp[:], T.wm[:], -2 * FAR, FAR, OP.mult, OP.add), "vco")
-    wait("s", "sco", "vco")
+    wait("s", "sco")
 
     for t in range(R):
         def B(name, u=t):
@@ -283,31 +291,37 @@ def rank_program(g, core, T, topo):
             for p in QUARTERS:
                 up(V.transpose(h(row, p, p + 32), h(block, a, a + 32, p=p)), sem)
 
-        def pack(u, v, sem):
-            n0 = NB * (R - 1 - u)
-            up(V.quantize_mx(B("mw", v)[:, n0:n0 + 130], B("mx", v)[:, n0:n0 + 130], B("nt", u)[:]), sem)
-
-        def filler(i):
-            if t:
-                number(i, 0)
-            elif i < 2:
-                c = R * NB + H * i
-                up(V.quantize_mx(T.mw1[:, c:c + H], T.mx1[:, c:c + H], T.met[:, 4 * H * i:4 * H * i + 4 * H]), "mc1")
+        def keep(q, u, v):
+            c = M + E * u
+            if q == "v":
+                up(V.tensor_copy(u32(s("mw", v), c, c + E), u32(s("nq", u), 0, 130).indirect(B("offs", u)[:, 0:2])),
+                   s("mc", v))
             else:
-                wait("v", "ldw")
-                up(V.quantize_mx(T.wq[:], T.wz[:], T.wt[:]), "wqd")
+                up(S.activation(B("mx", v)[:, c:c + E], B("nz", u)[:, 0:130].indirect(B("offs", u)[:, 0:2]), AF.Copy),
+                   s("mc", v))
+
+        def memory(i, sem):
+            up(V.tensor_copy(u32(s("mq", t + 1), H * i, H * i + H),
+                             u32(s("mw"), 0, MW).indirect(B("offm")[:, 8 * i:8 * i + 8])), s(sem))
+
+        def again(i, v):
+            up(V.quantize_mx(B("mw", v)[:, H * i:H * i + H], B("mx", v)[:, H * i:H * i + H],
+                             T.met[:, 4 * H * i:4 * H * i + 4 * H]), s("mc", v))
+
+        def cast(q, b):
+            wait(q, bank[b])
+            out, src = B("nt")[:, b:512:4], T.pbl[:, 512 * b:512 * b + NQ]
+            up(V.tensor_copy(out, src) if q == "v" else S.activation(out, src, AF.Copy), s("nt"))
 
         one = (0, 1)
         va, vb, vk, vc, vm, vr = s("va"), s("vb"), s("vk"), s("vc"), s("vm"), s("vr")
+        bank = {0: s("ba"), 1: s("bb"), 2: s("bc"), 3: s("bd")}
         mq, mz, qa, qz = B("mq"), B("mz"), B("qa"), B("qz")
         if t == 0:
             wait("t", "mq0", "oq", "op", "qx")
         else:
-            wait("t", s("mp", 0), s("mo", 0), s("rn", 0), s("qp", 0))
-        up(P.matmul_mx(T.psc[:, 0:H], qa[:], qz[:], mq[:, 0:H], mz[:, 0:H], True, True), s("sa"))
-        if t:
-            wait("t", s("m2", 0))
-        up(P.matmul_mx(T.psc[:, 512:512 + H], qa[:], qz[:], mq[:, H:M], mz[:, H:M], True, True), s("sb"))
+            wait("t", s("mp", 0), s("m2", 0), s("mo", 0), s("rn", 0), s("qp", 0))
+        up(P.matmul_mx(T.psc[:, 0:M], qa[:], qz[:], mq[:], mz[:], True, True), s("sa"))
         wait("t", "eqd")
         if t:
             wait("t", s("nt", 0))
@@ -317,12 +331,12 @@ def rank_program(g, core, T, topo):
         run, land, num, k = B("run"), B("land"), B("num"), 4 * rank
         top = run[:, M - 1:M]
         wait("v", s("sa"))
-        up(V.tensor_tensor_scan(run[:, 0:H], T.psc[:, 0:H], T.zz[:], LOW, OP.max, OP.add), s("ra"))
-        wait("v", s("sb"), s("ra"))
-        up(V.tensor_tensor_scan(run[:, H:M], T.psc[:, 512:512 + H], T.zz[:], run[:, H - 1:H], OP.max, OP.add), s("rn"))
+        up(V.tensor_tensor_scan(run[:], T.psc[:, 0:M], T.zz[:], LOW, OP.max, OP.add), s("rn"))
         wait("g", s("rn"))
         send((top, land[:, k:k + 1], off, common, s("ar")), (top, land[:, k:k + 1], [other], local, s("ar")))
         comes(s("ar"), (N - 1) * wide)
+        if t == 0:
+            up(g.iota(T.pl[:], [[int(FAR), M]], 0, 0, allow_small_or_imprecise_dtypes=True), "gi2")
         wait("s", s("rn"))
         up(S.activation(f("sg"), run[:, 0:M], AF.Sign, bias=top, scale=-1.0, accum_out=f("ti", *one)), s("ix"))
         up(S.activation(land[:, k:k + 1], top, AF.Copy), s("ow"))
@@ -332,158 +346,170 @@ def rank_program(g, core, T, topo):
         send((num[:, k:k + 1], num[:, k:k + 1], aides + [other], local, s("id")))
         comes(s("id"), (N - 1) * wide)
         if t == 0:
-            wait("v", "oq", "qx", "vco")
-            wait("s", "op", "qx")
+            up(g.iota(T.rst[:], [[0, 8], [-1, EK]], E, 0, allow_small_or_imprecise_dtypes=True), "gi3")
+            wait("v", "oq", "qx", "vco", "sco")
+            wait("s", "op", "qx", "vco")
             up(V.tensor_copy(u32("win0", NS, NS + NQ), u32("qa0", 0, NQ).indirect(T.idl[:, 0:8])), s("qc"))
+            up(V.tensor_scalar(T.wp[:], T.wm[:], -2 * FAR, FAR, OP.mult, OP.add), "vz")
             up(S.activation(T.wis0[:, NS:NS + NQ], T.qz0[:, 0:NQ].indirect(T.idl[:, 0:8]), AF.Copy), s("qc"))
         else:
             up(V.tensor_copy(u32("win1", NS, NS + NQ), u32("win0", 0, NS + NQ).indirect(T.offq0[:, 0:8])), s("qc"))
             up(S.activation(T.wis1[:, NS:NS + NQ], T.wis0[:, 0:NS + NQ].indirect(T.offq0[:, 0:8]), AF.Copy), s("qc"))
-            pack(0, 1, "mc1")
+            up(V.tensor_scalar(T.rst[:, 0:8 * EK:EK], f("am", E, 8 * EK, EK, 0), float(E), None, OP.add), "rs")
+        wait("v", s("rn"))
+        up(V.tensor_reduce(f("eps", 0, 1), top, AX, OP.max, apply_absolute_value=True), vr)
+        if rank > 0:
+            up(V.tensor_scalar(f("thr", 0, rank), T.zz[:, 0:rank], top, None, OP.add), s("ow"))
         wait("v", s("ix"))
         up(V.tensor_scalar(f("ra"), T.wm[:], f("ti", *one), None, OP.mult), va)
-        filler(0)
+        wait("v", vr)
+        up(V.tensor_scalar(f("eps", 1, 2), f("eps", 0, 1), STEP, TINY, OP.mult, OP.add), vr)
         wait("v", va)
         turn("la", "ra", va)
-        filler(1)
+        wait("v", vr)
+        up(V.tensor_scalar(f("thr", rank, N), T.zz[:, 0:N - rank], f("eps", 1, 2), top, OP.add, OP.add), s("ow"))
         wait("v", va)
         up(V.tensor_tensor_scan(h("ly"), T.nwm[0:32, :], h("la"), 0.0, OP.mult, OP.add), va)
-        filler(2)
+        if t:
+            number(0, 0)
+        else:
+            again(0, 0)
         wait("v", va)
         lanes(B("offi"), "ly", 0.0, s("oi"))
+        if t:
+            number(1, 0)
+            keep("v", 0, 1)
+        else:
+            again(1, 0)
         wait("v", s("oi"), "mp0", "m20")
         up(V.tensor_copy(u32(s("pm"), 0, NQ), u32(s("mq"), 0, M).indirect(B("offi")[:, 0:8])), s("pm"))
         wait("s", s("oi"))
         up(S.activation(B("pz")[:, 0:NQ], mz[:, 0:M].indirect(B("offi")[:, 0:8]), AF.Copy), s("pm"))
         ri = B("ri")
-
-        def places(i):
-            up(V.tensor_tensor(ri[:, 64 * i:64 * i + 64], T.pl[:, 0:M].indirect(B("offi")[:, 4 * i:4 * i + 4]),
-                               T.jr[:, NQ * t + 64 * i:NQ * t + 64 * i + 64], OP.add), s("rb"))
-
+        wait("s", "gi2")
+        up(S.activation(ri[:, 0:NQ], T.pl[:, 0:M].indirect(B("offi")[:, 0:8]), AF.Copy), s("rb"))
         wait("t", s("pm"))
-        bank = {0: s("ba"), 1: s("bb"), 2: s("bc"), 3: s("bd")}
         for b in (0, 1, 2, 3):
             up(P.matmul_mx(T.pbl[:, 512 * b:512 * b + NQ], T.eq[:, 128 * b:128 * b + 128], T.ez[:, 128 * b:128 * b + 128],
                            B("pm")[:], B("pz")[:], False, True), bank[b])
-        nt = B("nt")
-        for b in (0, 1, 2):
-            wait("s", bank[b])
-            up(S.activation(nt[:, b:512:4], T.pbl[:, 512 * b:512 * b + NQ], AF.Copy), s("nt"))
-        wait("v", "gi2")
-        places(0)
-        wait("v", s("ar"))
-        if rank > 0:
-            up(V.tensor_scalar(f("wn", 0, rank), land[:, 0:k:4], top, WON, OP.is_lt, OP.mult), vb)
-        if rank < N - 1:
-            up(V.tensor_scalar(f("wn", rank + 1, N), land[:, k + 4:32:4], top, WON, OP.is_le, OP.mult), vb)
-        wait("v", s("ow"))
+        cast("s", 0)
+        cast("s", 2)
+        wait("v", "gi2", s("ow"), s("ar"))
+        up(V.tensor_tensor(f("wn", 0, N), land[:, 0:32:4], f("thr"), OP.is_lt), vb)
         up(V.tensor_tensor_scan(f("rl"), land[:, 0:32:4], T.zz[:, 0:8], LOW, OP.max, OP.add), vr)
-        places(1)
+        if t:
+            number(2, 0)
         wait("v", vb)
-        up(V.tensor_tensor_scan(f("fr", 0, 40), f("wn", 0, 40), f("wn", 0, 40), WON, OP.max, OP.max), vb)
+        up(V.tensor_tensor_scan(f("fr", 0, 40), f("wn", 0, 40), T.dn[:, 0:40], WON, OP.min, OP.mult), vb)
         wait("v", vr)
         up(V.tensor_scalar(f("sl", 1, N + 1), f("rl"), f("rl", 7, 8), None, OP.is_ge), vr)
         wait("v", vb)
         turn("ft", "fr", vb, 8)
+        cast("v", 1)
         wait("v", vr)
         up(V.tensor_tensor(f("oh", 0, N), f("sl", 1, N + 1), f("sl", 0, N), OP.subtract), vc)
-        up(V.tensor_tensor_scan(f("cb", 12, 37, 3), T.tb[:, 0:N + 1], f("sl", 1, N + 2), 0.0, OP.add, OP.mult), vr)
         wait("v", vb)
-        up(V.tensor_tensor_scan(h("sa"), h("ft"), T.one[0:32, :], T.cst[0:32, 9:10], OP.add, OP.add), vb)
-        up(V.tensor_tensor_scan(h("sb"), h("ft"), T.one[0:32, :], T.cst[0:32, 10:11], OP.add, OP.add), s("ac"))
-        wait("v", bank[3])
-        up(V.tensor_copy(nt[:, 3:512:4], T.pbl[:, 1536:1536 + NQ]), s("nt"))
+        up(V.tensor_tensor_scan(h("sa"), h("ft"), T.down[0:32, :], T.ini[0:32, 0:1], OP.add, OP.min), vb)
+        up(V.tensor_tensor_scan(h("sb"), h("ft"), T.down[0:32, :], T.ini[0:32, 2:3], OP.add, OP.min), s("ac"))
+        cast("v", 3)
         wait("v", vb)
-        up(V.tensor_reduce(h("acc", 0, 1), h("sa"), AX, OP.min, apply_absolute_value=True), vb)
+        up(V.tensor_tensor_scan(h("sc", 0, NQ), h("sa"), h("sa"), -1.0, OP.max, OP.max), vb)
         wait("v", s("ac"))
-        up(V.tensor_reduce(h("acc", 1, 2), h("sb"), AX, OP.min, apply_absolute_value=True), vb)
+        up(V.tensor_tensor_scan(h("sc", NQ, 2 * NQ), h("sb"), h("sb"), -1.0, OP.max, OP.max), vb)
         wait("v", s("nt"))
-        pack(t, t, s("nq"))
+        up(V.quantize_mx(B("nq")[:, 0:130], B("nz")[:, 0:130], B("nt")[:]), s("nq"))
         wait("v", vb)
-        offs, n0, e = B("offs"), NB * (R - 1 - t), slot(core)
+        offs, e = B("offs"), slot(core)
         for p in QUARTERS:
-            up(V.tensor_scalar(offs[p:p + 32, 0:2], h("acc", 0, 2), NQ + 1.0, -1.0, OP.min, OP.add), s("os"))
+            up(V.tensor_scalar(offs[p:p + 32, 0:2], h("sc", NQ - 1, 2 * NQ, NQ), -1.0, NQ - 1.0, OP.mult, OP.add), s("os"))
         wait("v", vc)
         up(V.tensor_tensor(f("dd", 0, 32, 4), f("oh", 0, N), f("oh", 1, N + 1), OP.subtract), vc)
+        up(V.tensor_tensor_scan(f("cb", 12, 37, 3), T.tb[:, 0:N + 1], f("sl", 1, N + 2), 0.0, OP.add, OP.mult), vr)
         wait("v", s("os"), s("nq"))
-        up(V.tensor_copy(u32(s("win"), e, e + E), u32(s("mw"), n0, n0 + 130).indirect(offs[:, 0:2])), s("sl"))
+        up(V.tensor_copy(u32(s("win"), e, e + E), u32(s("nq"), 0, 130).indirect(offs[:, 0:2])), s("sl"))
         wait("s", s("nq"), s("os"))
-        up(S.activation(B("wis")[:, e:e + E], B("mx")[:, n0:n0 + 130].indirect(offs[:, 0:2]), AF.Copy), s("sz"))
+        up(S.activation(B("wis")[:, e:e + E], B("nz")[:, 0:130].indirect(offs[:, 0:2]), AF.Copy), s("sz"))
         codes, planes = u8(s("win"), e, e + E), B("wis")[:, e:e + E]
         wait("g", s("sz"))
-        send((planes, planes, aides[:1], common, s("nb")), (planes, planes, aides[1:] + [other], local, s("nb")))
+        send((planes, planes, aides, common, s("nb")), (planes, planes, helpers(other) + [other], local, s("nb")))
         wait("g", s("sl"))
-        send((codes, codes, far[:1], common, s("na")), (codes, codes, [other], local, s("nx")))
-        send((codes, codes, plane + mates, common, s("nx")))
-        comes(s("na"), wide)
-        comes(s("nb"), (N - 1) * wide)
-        comes(s("nx"), (N - 2) * wide)
-        wait("g", s("na"))
-        came = u8(s("win"), slot(far[0]), slot(far[0]) + E)
-        send((came, came, [other], local, s("nx")))
+        send((codes, codes, off, common, s("nx")), (codes, codes, [other], local, s("nx")))
+        comes(s("nb"), (1 + len(same)) * wide)
+        comes(s("nx"), (N - 1) * wide)
         wait("s", s("rb"))
         for c in range(8):
-            up(S.activation(f("ab", E * c, E * c + E), ri[:, 0:RI].indirect(offs[:, 0:2]), AF.Abs, bias=T.cn[:, c:c + 1],
-                            scale=1.0), s("ab"))
+            up(S.activation(f("ab", EK * c + 1, EK * c + EK), ri[:, 0:RI].indirect(offs[:, 0:2]), AF.Abs,
+                            bias=T.cn[:, c:c + 1], scale=1.0), s("ab"))
         wait("v", vc)
         turn("ot", "dd", vk)
+        keep("v", t, t)
+        keep("s", t, t)
+        if t:
+            keep("s", 0, 1)
         wait("v", vk)
-        up(V.tensor_tensor_scan(h("ct"), h("ot"), T.zz[0:32, :], 0.0, OP.add, OP.add), vc)
+        up(V.tensor_tensor_scan(h("ct"), h("ot"), T.zz[0:32, 0:NQ], 0.0, OP.add, OP.add), vc)
+        if t:
+            wait("v", "ldw")
+            up(V.quantize_mx(T.wq[:], T.wz[:], T.wt[:]), "wqd")
+        else:
+            wait("v", "gi3")
+            for i, p in enumerate(HALVES):
+                up(V.tensor_scalar(T.rst[p:p + 64, 0:8 * EK:EK], T.cp[p:p + 64, 8 * i:8 * i + 8], -1.0, M + E - 1.0,
+                                   OP.mult, OP.add), "rs")
         wait("v", vc, vr)
         for p in QUARTERS:
             up(V.transpose(h("cb", 0, 32, p=p), h("ct", p, p + 32)), vc)
         wait("v", vc)
         up(V.tensor_tensor_scan(f("kk", 0, 11), f("cb", 0, 44, 4), f("sl", 1, N + 4), 0.0, OP.add, OP.mult), vc)
-        wait("v", s("ab"))
-        up(V.tensor_tensor_scan(f("am"), T.rst[:], f("ab"), 0.0, OP.max, OP.min), vm)
+        wait("v", s("ab"), "rs", "vz")
+        up(V.tensor_tensor_scan(f("am"), f("ab"), T.rst[:], 0.0, OP.min, OP.max), vm)
         wait("v", vc)
         up(V.tensor_scalar(f("rc"), T.wp[:], f("kk", 8, 9), f("kk", 10, 11), OP.max, OP.max), vc)
 
         def spread(p):
             for i, q in enumerate(HALVES):
-                up(V.tensor_copy(B("offm")[p:p + 64, 8 * i:8 * i + 8], h("am", 31, 256, 32, p=q, n=64)), s("om"))
+                up(V.tensor_scalar(B("offm")[p:p + 64, 8 * i:8 * i + 8], h("am", E, 8 * EK, EK, p=q, n=64), -1.0,
+                                   M + E * (t + 1) - 1.0, OP.mult, OP.add), s("om"))
 
-        wait("v", vm)
         if t:
-            up(V.tensor_tensor(f("am", 31, 256, 32), f("am", 31, 256, 32), f("am", 31, 256, 32, 0), OP.min), vm)
             number(0, 1)
         else:
-            spread(0)
-            spread(64)
-        wait("v", vc)
-        turn("lc", "rc", vc)
-        if t:
             wait("v", vm)
             spread(0)
-        else:
-            wait("v", s("om"), s("mc"))
-            up(V.tensor_copy(u32(s("mq", t + 1), 0, H), u32(s("mw"), 0, MW).indirect(B("offm")[:, 0:8])), s("mp"))
+        wait("v", vc)
+        turn("lc", "rc", vc)
+        wait("v", vm)
+        spread(0 if t else 64)
         wait("v", vc)
         up(V.tensor_tensor_scan(h("oy"), T.old[0:32, :], h("lc"), -FAR, OP.max, OP.min), vc)
         if t:
             spread(64)
             number(1, 1)
+        else:
+            wait("v", s("om"), s("mc"))
+            memory(0, "mp")
         wait("v", vc)
         lanes(B("offq"), "oy", float(NS), s("od"))
         if t:
             number(2, 1)
+        else:
+            memory(1, "m2")
         wait("s", s("om"), s("mc"))
         for i in range(2):
             up(S.activation(B("mz", t + 1)[:, H * i:H * i + H], B("mx")[:, 0:MW].indirect(B("offm")[:, 8 * i:8 * i + 8]),
                             AF.Copy), s("mo"))
-            if t and i == 0:
-                wait("s", s("od"), s("sz"), s("qc"), s("nb"))
-                up(S.activation(T.qz2[:, 0:NQ], B("wis")[:, 0:NS + NQ].indirect(B("offq")[:, 0:8]), AF.Copy), s("qp"))
-        wait("v", s("od"), s("sl"), s("qc"), s("na"), s("nx"))
-        up(V.tensor_copy(u32(s("qa", t + 1), 0, NQ), u32(s("win"), 0, NS + NQ).indirect(B("offq")[:, 0:8])), s("qp"))
+        wait("s", s("od"), s("sz"), s("qc"), s("nb"))
+        up(S.activation(B("qz", t + 1)[:, 0:NQ], B("wis")[:, 0:NS + NQ].indirect(B("offq")[:, 0:8]), AF.Copy), s("qp"))
         if t:
             wait("v", s("om"), s("mc"))
-            up(V.tensor_copy(u32(s("mq", t + 1), 0, H), u32(s("mw"), 0, MW).indirect(B("offm")[:, 0:8])), s("mp"))
+            memory(0, "mp")
+        wait("v", s("od"), s("sl"), s("qc"), s("nx"))
+        up(V.tensor_copy(u32(s("qa", t + 1), 0, NQ), u32(s("win"), 0, NS + NQ).indirect(B("offq")[:, 0:8])), s("qp"))
+        if t:
+            memory(1, "m2")
         else:
-            wait("s", s("od"), s("sz"), s("qc"), s("nb"))
-            up(S.activation(T.qz1[:, 0:NQ], B("wis")[:, 0:NS + NQ].indirect(B("offq")[:, 0:8]), AF.Copy), s("qp"))
-        up(V.tensor_copy(u32(s("mq", t + 1), H, M), u32(s("mw"), 0, MW).indirect(B("offm")[:, 8:16])), s("m2"))
+            again(0, 1)
+            again(1, 1)
 
     wait("y", "wi0", "wi1")
     for u in range(R):

from concourse.bass import DstId, RemoteDMATransfer
from concourse.mybir import dt, AluOpType, AxisListType, ActivationFunctionType

N, M, A, E, R = 8, 256, 16, 32, 2
NQ = N * A
NS = N * E
H = M // 2
OP = AluOpType
AF = ActivationFunctionType
AX = AxisListType.X
LOW = -9.0e29
FAR = 1024.0
WON = 256.0
STEP = 1.25 * 2.0 ** -24
TINY = 1.0e-37
MW = M + R * E
EK = E + 1
RI = NQ + 8

WORK = [("ti", 8), ("eps", 8), ("thr", 8), ("rl", 8), ("kk", 16), ("ol", 8), ("ix", 8), ("b2", 8),
        ("sg", 256), ("ab", 8 * EK), ("am", 8 * EK)]
HALF = [("wn", 48), ("oh", 16), ("dd", 32), ("cb", 48), ("sl", 16),
        ("ra", 32), ("la", 128), ("ly", 128), ("fr", 48), ("ft", 128), ("sa", 128), ("sb", 128), ("sc", 256),
        ("ot", 128), ("ct", 128), ("rc", 32), ("lc", 128), ("oy", 128)]
AT = {}
_n = {}
for _b, _l in (("f", WORK), ("h", HALF)):
    _n[_b] = 0
    for _name, _w in _l:
        AT[_name] = (_b, _n[_b], _w)
        _n[_b] += _w
PRE = AT["ra"][1]

SCRATCH = {
    "xt": ("sbuf", [128, 512], "bfloat16"), "met": ("sbuf", [128, 4 * M], "bfloat16"),
    "wt": ("sbuf", [128, 512], "bfloat16"), "et": ("sbuf", [128, 520], "bfloat16"),
    "half": ("sbuf", [128, 128], "bfloat16"), "diag": ("sbuf", [128, 128], "bfloat16"),
    "xq": ("sbuf", [128, 160], "float8_e4m3fn_x4"), "xs": ("sbuf", [128, 160], "uint8"),
    "wq": ("sbuf", [128, 128], "float8_e4m3fn_x4"), "wz": ("sbuf", [128, 128], "uint8"),
    "eq": ("sbuf", [128, 512], "float8_e4m3fn_x4"), "ez": ("sbuf", [128, 512], "uint8"),
    "zz": ("sbuf", [128, M], "bfloat16"), "down": ("sbuf", [128, 128], "bfloat16"), "dn": ("sbuf", [128, 48], "bfloat16"),
    "wm": ("sbuf", [128, 32], "bfloat16"), "nwm": ("sbuf", [128, 128], "bfloat16"), "ini": ("sbuf", [128, 8], "bfloat16"),
    "wp": ("sbuf", [128, 32], "bfloat16"), "old": ("sbuf", [128, 128], "bfloat16"), "tb": ("sbuf", [128, 16], "float32"),
    "rst": ("sbuf", [128, 8 * EK], "float32"), "im": ("sbuf", [128, 128], "float32"), "pl": ("sbuf", [128, M], "float32"),
    "ip": ("sbuf", [128, 8], "int32"), "ia": ("sbuf", [128, 8], "int32"),
    "c16": ("sbuf", [128, 16], "float32"), "cp": ("sbuf", [128, 16], "float32"),
    "cn": ("sbuf", [128, 8], "float32"),
    "cst": ("sbuf", [128, 8], "float32"), "yt": ("sbuf", [128, 128], "float32"),
    "idl": ("sbuf", [128, 16], "uint16"),
    "psc": ("psum", [128, 512], "float32"), "pbl": ("psum", [128, 2048], "float32"), "pyy": ("psum", [128, 512], "float32"),
}
for _t in range(R + 1):
    SCRATCH["mq%d" % _t] = ("sbuf", [128, M], "float8_e4m3fn_x4")
    SCRATCH["mz%d" % _t] = ("sbuf", [128, M], "uint8")
    SCRATCH["qa%d" % _t] = ("sbuf", [128, NQ], "float8_e4m3fn_x4")
    SCRATCH["qz%d" % _t] = ("sbuf", [128, NQ], "uint8")
for _t in range(R):
    for _name, _w, _d in (("mw", MW, "float8_e4m3fn_x4"), ("mx", MW, "uint8"),
                          ("win", NS + NQ, "float8_e4m3fn_x4"), ("wis", NS + NQ, "uint8"),
                          ("pm", NQ, "float8_e4m3fn_x4"), ("pz", NQ, "uint8"),
                          ("nq", 160, "float8_e4m3fn_x4"), ("nz", 160, "uint8"),
                          ("nt", 520, "bfloat16"), ("run", M, "float32"), ("land", 32, "float32"), ("num", 32, "float32"),
                          ("ri", RI, "float32"), ("wv", 8, "float32"),
                          ("f", _n["f"], "float32"), ("h", _n["h"], "bfloat16"),
                          ("offi", 8, "uint16"), ("offs", 2, "uint16"), ("offm", 16, "uint16"), ("offq", 8, "uint16")):
        SCRATCH["%s%d" % (_name, _t)] = ("sbuf", [128, _w], _d)

ONCE = ["ldx", "ldm", "ldw", "ixt", "ihf", "gdi", "gip", "gi1", "gi2", "gi3", "xqd", "eqd", "wqd", "qx", "px", "vz", "oq",
        "op", "mq0", "vcc", "vco", "vid", "ls", "yp", "yc", "st", "sty", "sco", "rs", "pre"]
EACH = ["sa", "rn", "ix", "ow", "oi", "pm", "ba", "bb", "bc", "bd", "nt", "nq", "ar", "ac", "os", "sl",
        "sz", "ab", "om", "mp", "mo", "od", "nx", "qp", "qc", "wi", "va", "vb", "vk", "vc", "vm", "vw",
        "nb", "rb", "ni", "id", "vr", "m2", "mc"]
SEMAPHORES = ONCE + ["%s%d" % (_s, _t) for _s in EACH for _t in range(R)]
QUARTERS = (0, 32, 64, 96)
HALVES = (0, 64)


def rank_program(g, core, T, topo):
    def partner(c):
        return [d for d in T.cores if d != c and topo.chip(d) == topo.chip(c)][0]

    def helpers(c):
        idle = [d for d in topo.cores_of(c) if d not in T.cores and topo.die(d) == topo.die(c)]
        port = [d for d in idle if all(topo.may_write(d, r) for r in T.cores)][0]
        return [port, [d for d in idle if d != port][0]]

    def slot(d):
        return NS - E * (T.rank_of(d) + 1)

    def bits(m):
        return sum(m >> e & 1 for e in range(m.bit_length()))

    rank = T.rank_of(core)
    served = [c for c in T.cores if core in helpers(c)]
    if rank is None and not served:
        return
    V, S, P, Y = g.vector, g.scalar, g.tensor, g.sync
    queue = {"v": V, "s": S, "t": P, "y": Y, "g": g}
    total, seen = {}, {}

    def comes(name, n):
        total[name] = total.get(name, 0) + n

    def up(ins, name, n=1):
        ins.then_inc(T.sem[name], n)
        comes(name, n)

    def wait(q, *names):
        for name in names:
            if seen.get((q, name), 0) < total.get(name, 0):
                queue[q].wait_ge(T.sem[name], total[name])
                seen[(q, name)] = total[name]
                seen[("", name)] = total[name]

    def rest():
        for name in total:
            if seen.get(("", name), 0) < total[name]:
                wait("g", name)

    def u32(name, a, b):
        return T[name][:, a:b].bitcast(dt.uint32)

    def u8(name, a, b):
        return T[name][:, a:b].bitcast(dt.uint8)

    here = topo.chip(core)

    def near(c):
        k = topo.chip(c)
        return (2 if topo.mates(here, k) else 1 if topo.same_plane(here, k) else 0, topo.die(c) != topo.die(core))

    off = sorted([c for c in T.cores if topo.chip(c) != here], key=near)
    plane = [c for c in off if near(c)[0] == 1]
    across = [c for c in off if c not in plane]
    same = [c for c in off if topo.die(c) == topo.die(core)]
    common = topo.mask(core, off[0])
    for c in off:
        common = common & topo.mask(core, c)
    wide = bits(common)

    def dst(c):
        rid, pid = topo.addr(c)[:2]
        return DstId(rid=rid, pnc=pid)

    def send(*parts):
        g.remote_dma_fused([
            RemoteDMATransfer(dst_ids=[dst(c) for c in to], dma_engine_mask=mask, remote_sem=T.sem[sem],
                              srcs=[src], dsts=[out for c in to]) for src, out, to, mask, sem in parts],
            local_sem=T.sem["ls"])
        for src, out, to, mask, sem in parts:
            comes("ls", bits(mask))

    if rank is None:
        boss = served[0]
        k, e = 4 * T.rank_of(boss), slot(boss)
        to = across if core == helpers(boss)[0] else plane
        c = min(e, slot(partner(boss)))
        for t in range(R):
            num, pln = T["num%d" % t][:, k:k + 1], T["wis%d" % t][:, c:c + 2 * E]
            comes("id%d" % t, wide)
            wait("g", "id%d" % t)
            send((num, num, to, common, "id%d" % t))
            comes("nb%d" % t, 2 * wide)
            wait("g", "nb%d" % t)
            send((pln, pln, [d for d in to if d in same], common, "nb%d" % t))
        rest()
        return

    other, aides = partner(core), helpers(core)
    local = topo.mask(core, other) & ~common
    lower = rank < T.rank_of(other)
    x0 = NQ - A if lower else 0
    q0 = A if lower else 2 * A
    own = q0 + x0

    up(Y.dma_start(T.xt[:, 4 * x0:4 * x0 + 4 * A], T.x[:]), "ldx", 16)
    up(Y.dma_start(T.met[:], T.me[:]), "ldm", 16)
    up(Y.dma_start(T.wt[:], T.w[:]), "ldw", 16)

    up(V.memset(T.xt[:, 0:4 * x0] if lower else T.xt[:, 4 * A:512], 0.0), "ixt")
    up(V.memset(T.half[:], 0.5), "ihf")
    up(g.iota(T.ip[:, 0:1], [[1, 1]], 0, 1), "gip")
    up(g.iota(T.c16[:], [[16, 16]], 0, 0, allow_small_or_imprecise_dtypes=True), "gip")
    wait("g", "ihf")
    up(g.affine_select(T.diag[:], T.half[:], [[-1, 128]], OP.is_equal, 0.0, 0, 1), "gdi")
    up(V.memset(T.zz[:], 0.0), "vz")
    wait("v", "gip")
    up(V.tensor_scalar(T.ia[:, 0:1], T.ip[:, 0:1], 15, None, OP.bitwise_and), "vid")
    up(V.memset(T.h0[:, 0:PRE], 0.0), "vz")
    wait("v", "vid")
    up(V.tensor_copy(T.cst[:, 1:2], T.ia[:, 0:1]), "vid")

    wait("v", "ldx", "ixt")
    up(V.quantize_mx(T.xq[:, q0:q0 + NQ], T.xs[:, q0:q0 + NQ], T.xt[:]), "xqd")
    a = A * rank
    wait("g", "xqd")
    xc, xp = u8("xq", own, own + A), T.xs[:, own:own + A]
    there = A if lower else NQ + A
    send((xp, T.xs[:, there:there + A], [other], common, "px"))
    send((xc, u8("qa0", a, a + A), off, common, "qx"))
    send((xc, u8("qa0", a, a + A), [other], local, "qx"))
    send((xp, T.qz0[:, a:a + A], [other], local, "qx"))
    comes("px", wide)
    comes("qx", (len(off) + 2 + len(same)) * wide)
    b = min(a, A * T.rank_of(other))
    both = own if lower else own - A
    wait("g", "px")
    send((T.xs[:, both:both + 2 * A], T.qz0[:, b:b + 2 * A], same, common, "qx"))
    up(g.iota(T.im[:], [[0, 8], [1, 16]], 0, 0, allow_small_or_imprecise_dtypes=True), "gi1")
    up(g.iota(T.down[0:32, :], [[-1, NQ]], NQ - 1, 0, allow_small_or_imprecise_dtypes=True), "gi2")

    up(V.memset(T.et[:], 0.0), "vcc")
    wait("v", "vid", "vz")
    up(V.tensor_scalar(T.cp[:], T.c16[:], T.cst[:, 1:2], None, OP.add), "vid")
    up(V.memset(T.old[:], -FAR), "rs")
    wait("v", "vcc", "gdi")
    up(V.tensor_copy(T.et[:, 3:515:4], T.diag[:]), "vcc")
    wait("v", "vid")
    up(V.tensor_copy(T.idl[:], T.cp[:]), "vid")

    def fill(out, n, value):
        up(S.activation(out, T.zz[:, 0:n], AF.Identity, bias=value), "sco")

    wait("s", "vz", "vid", "xqd")
    up(S.activation(T.qz0[:, a:a + A], T.xs[:, own:own + A].indirect(T.idl[:, 0:1]), AF.Copy), "op")
    for c in range(2):
        up(S.activation(T.ini[:, 2 * c:2 * c + 1], T.cst[:, 1:2], AF.Identity, bias=NQ - WON * (E - 16 * c), scale=WON),
           "sco")
    for i, p in enumerate(HALVES):
        up(S.activation(T.cn[p:p + 64, 0:8], T.cp[p:p + 64, 8 * i:8 * i + 8], AF.Copy, scale=-FAR), "sco")
    wait("s", "rs")
    up(S.activation(T.old[:, 0:128:16], T.cp[:, 0:8], AF.Copy), "sco")
    fill(T.tb[:, 0:N], N, -float(E))
    fill(T.tb[:, N:N + 1], 1, float(NS))

    for name, n, m, value in (("wn", 0, 48, WON), ("sl", N + 1, N + 2, FAR), ("sl", N + 2, N + 3, 1.0),
                              ("sl", N + 3, N + 4, -1.0 / FAR), ("cb", 32, 33, -E - 0.5), ("cb", 40, 41, (E + 0.5) * FAR)):
        o = AT[name][1]
        up(V.memset(T.h0[:, o + n:o + m], value), "pre")
    wait("v", "vid", "xqd", "vcc")
    up(V.tensor_copy(u32("qa0", a, a + A), u32("xq", own, own + A).indirect(T.idl[:, 0:1])), "oq")
    for b in range(4):
        up(V.quantize_mx(T.eq[:, 128 * b:128 * b + 128], T.ez[:, 128 * b:128 * b + 128], T.et[:, 3 - b:515 - b]), "eqd")
    wait("v", "pre")
    up(V.tensor_copy(T.h1[:, 0:PRE], T.h0[:, 0:PRE]), "vco")
    wait("v", "ldm")
    up(V.quantize_mx(T.mq0[:], T.mz0[:], T.met[:]), "mq0")
    o = AT["ab"][1]
    for t in range(R):
        up(V.memset(T["ri%d" % t][:, NQ:RI], 1000.0 * FAR), "vco")
        up(V.memset(T["f%d" % t][:, o:o + 8 * EK:EK], 0.0), "vco")
        up(V.memset(T["nt%d" % t][:, 512:520], 0.0), "vco")
    for n, m, value in ((0, N, 1.0), (N, N + 1, WON), (N + 1, 48, 1.0)):
        up(V.memset(T.dn[:, n:m], value), "vco")
    wait("v", "gi1")
    up(V.tensor_scalar(T.wm[:], T.im[:, 0:32], T.cst[:, 1:2], None, OP.is_equal), "vco")
    up(V.tensor_scalar(T.nwm[:], T.im[:], T.cst[:, 1:2], None, OP.not_equal), "vco")
    wait("s", "sco")

    for t in range(R):
        def B(name, u=t):
            return T["%s%d" % (name, u)]

        def s(name, u=t):
            return "%s%d" % (name, u)

        def h(name, a=0, b=None, step=1, p=0, n=32, u=t):
            buf, o, w = AT[name]
            return B(buf, u)[p:p + n, o + a:o + (w if b is None else b):step]

        def f(name, a=0, b=None, step=1, u=t):
            return h(name, a, b, step, 0, 128, u)

        def lanes(out, y, more, sem):
            for p in QUARTERS:
                up(V.tensor_scalar(out[p:p + 32, 0:8], h(y, 15, 128, 16), more, None, OP.add), sem)

        def number(step, u=t):
            one, vw = (0, 1, 1, u), s("vw", u)
            wait("v", vw)
            if step == 0:
                up(V.tensor_scalar(f("b2", *one), f("kk", 7, 8, 1, u), E + 0.5, 0.5, OP.is_lt, OP.subtract), vw)
                wait("v", s("id", u), s("ni", u))
                up(V.tensor_tensor(f("ol", 0, 8, 1, u), f("oh", 0, 8, 1, u), B("num", u)[:, 0:32:4], OP.mult), vw)
            elif step == 1:
                up(V.tensor_reduce(f("ix", *one), f("ol", 0, 8, 1, u), AX, OP.add), vw)
            else:
                up(V.tensor_scalar(B("wv", u)[:, 0:1], f("ix", *one), f("b2", *one), -0.5, OP.mult, OP.add), s("wi", u))

        def turn(row, block, sem, a=0):
            for p in QUARTERS:
                up(V.transpose(h(row, p, p + 32), h(block, a, a + 32, p=p)), sem)

        def keep(q, u, v):
            c = M + E * u
            if q == "v":
                up(V.tensor_copy(u32(s("mw", v), c, c + E), u32(s("nq", u), 0, 130).indirect(B("offs", u)[:, 0:2])),
                   s("mc", v))
            else:
                up(S.activation(B("mx", v)[:, c:c + E], B("nz", u)[:, 0:130].indirect(B("offs", u)[:, 0:2]), AF.Copy),
                   s("mc", v))

        def memory(i, sem):
            up(V.tensor_copy(u32(s("mq", t + 1), H * i, H * i + H),
                             u32(s("mw"), 0, MW).indirect(B("offm")[:, 8 * i:8 * i + 8])), s(sem))

        def again(i, v):
            up(V.quantize_mx(B("mw", v)[:, H * i:H * i + H], B("mx", v)[:, H * i:H * i + H],
                             T.met[:, 4 * H * i:4 * H * i + 4 * H]), s("mc", v))

        def cast(q, b):
            wait(q, bank[b])
            out, src = B("nt")[:, b:512:4], T.pbl[:, 512 * b:512 * b + NQ]
            up(V.tensor_copy(out, src) if q == "v" else S.activation(out, src, AF.Copy), s("nt"))

        one = (0, 1)
        va, vb, vk, vc, vm, vr = s("va"), s("vb"), s("vk"), s("vc"), s("vm"), s("vr")
        bank = {0: s("ba"), 1: s("bb"), 2: s("bc"), 3: s("bd")}
        mq, mz, qa, qz = B("mq"), B("mz"), B("qa"), B("qz")
        if t == 0:
            wait("t", "mq0", "oq", "op", "qx")
        else:
            wait("t", s("mp", 0), s("m2", 0), s("mo", 0), s("rn", 0), s("qp", 0))
        up(P.matmul_mx(T.psc[:, 0:M], qa[:], qz[:], mq[:], mz[:], True, True), s("sa"))
        wait("t", "eqd")
        if t:
            wait("t", s("nt", 0))
        for b in (0, 1, 2, 3):
            P.matmul_mx(T.pbl[:, 512 * b:512 * b + NQ], T.eq[:, 128 * b:128 * b + 128], T.ez[:, 128 * b:128 * b + 128],
                        qa[:], qz[:], True, False)
        run, land, num, k = B("run"), B("land"), B("num"), 4 * rank
        top = run[:, M - 1:M]
        wait("v", s("sa"))
        up(V.tensor_tensor_scan(run[:], T.psc[:, 0:M], T.zz[:], LOW, OP.max, OP.add), s("rn"))
        wait("g", s("rn"))
        send((top, land[:, k:k + 1], off, common, s("ar")), (top, land[:, k:k + 1], [other], local, s("ar")))
        comes(s("ar"), (N - 1) * wide)
        if t == 0:
            up(g.iota(T.pl[:], [[int(FAR), M]], 0, 0, allow_small_or_imprecise_dtypes=True), "gi2")
        wait("s", s("rn"))
        up(S.activation(f("sg"), run[:, 0:M], AF.Sign, bias=top, scale=-1.0, accum_out=f("ti", *one)), s("ix"))
        up(S.activation(land[:, k:k + 1], top, AF.Copy), s("ow"))
        wait("s", s("ix"))
        up(S.activation(num[:, k:k + 1], f("ti", *one), AF.Identity, bias=2.0 * M * rank + 1.0, scale=2.0), s("ni"))
        wait("g", s("ni"))
        send((num[:, k:k + 1], num[:, k:k + 1], aides + [other], local, s("id")))
        comes(s("id"), (N - 1) * wide)
        if t == 0:
            up(g.iota(T.rst[:], [[0, 8], [-1, EK]], E, 0, allow_small_or_imprecise_dtypes=True), "gi3")
            wait("v", "oq", "qx", "vco", "sco")
            wait("s", "op", "qx", "vco")
            up(V.tensor_copy(u32("win0", NS, NS + NQ), u32("qa0", 0, NQ).indirect(T.idl[:, 0:8])), s("qc"))
            up(V.tensor_scalar(T.wp[:], T.wm[:], -2 * FAR, FAR, OP.mult, OP.add), "vz")
            up(S.activation(T.wis0[:, NS:NS + NQ], T.qz0[:, 0:NQ].indirect(T.idl[:, 0:8]), AF.Copy), s("qc"))
        else:
            up(V.tensor_copy(u32("win1", NS, NS + NQ), u32("win0", 0, NS + NQ).indirect(T.offq0[:, 0:8])), s("qc"))
            up(S.activation(T.wis1[:, NS:NS + NQ], T.wis0[:, 0:NS + NQ].indirect(T.offq0[:, 0:8]), AF.Copy), s("qc"))
            up(V.tensor_scalar(T.rst[:, 0:8 * EK:EK], f("am", E, 8 * EK, EK, 0), float(E), None, OP.add), "rs")
        wait("v", s("rn"))
        up(V.tensor_reduce(f("eps", 0, 1), top, AX, OP.max, apply_absolute_value=True), vr)
        if rank > 0:
            up(V.tensor_scalar(f("thr", 0, rank), T.zz[:, 0:rank], top, None, OP.add), s("ow"))
        wait("v", s("ix"))
        up(V.tensor_scalar(f("ra"), T.wm[:], f("ti", *one), None, OP.mult), va)
        wait("v", vr)
        up(V.tensor_scalar(f("eps", 1, 2), f("eps", 0, 1), STEP, TINY, OP.mult, OP.add), vr)
        wait("v", va)
        turn("la", "ra", va)
        wait("v", vr)
        up(V.tensor_scalar(f("thr", rank, N), T.zz[:, 0:N - rank], f("eps", 1, 2), top, OP.add, OP.add), s("ow"))
        wait("v", va)
        up(V.tensor_tensor_scan(h("ly"), T.nwm[0:32, :], h("la"), 0.0, OP.mult, OP.add), va)
        if t:
            number(0, 0)
        else:
            again(0, 0)
        wait("v", va)
        lanes(B("offi"), "ly", 0.0, s("oi"))
        if t:
            number(1, 0)
            keep("v", 0, 1)
        else:
            again(1, 0)
        wait("v", s("oi"), "mp0", "m20")
        up(V.tensor_copy(u32(s("pm"), 0, NQ), u32(s("mq"), 0, M).indirect(B("offi")[:, 0:8])), s("pm"))
        wait("s", s("oi"))
        up(S.activation(B("pz")[:, 0:NQ], mz[:, 0:M].indirect(B("offi")[:, 0:8]), AF.Copy), s("pm"))
        ri = B("ri")
        wait("s", "gi2")
        up(S.activation(ri[:, 0:NQ], T.pl[:, 0:M].indirect(B("offi")[:, 0:8]), AF.Copy), s("rb"))
        wait("t", s("pm"))
        for b in (0, 1, 2, 3):
            up(P.matmul_mx(T.pbl[:, 512 * b:512 * b + NQ], T.eq[:, 128 * b:128 * b + 128], T.ez[:, 128 * b:128 * b + 128],
                           B("pm")[:], B("pz")[:], False, True), bank[b])
        cast("s", 0)
        cast("s", 2)
        wait("v", "gi2", s("ow"), s("ar"))
        up(V.tensor_tensor(f("wn", 0, N), land[:, 0:32:4], f("thr"), OP.is_lt), vb)
        up(V.tensor_tensor_scan(f("rl"), land[:, 0:32:4], T.zz[:, 0:8], LOW, OP.max, OP.add), vr)
        if t:
            number(2, 0)
        wait("v", vb)
        up(V.tensor_tensor_scan(f("fr", 0, 40), f("wn", 0, 40), T.dn[:, 0:40], WON, OP.min, OP.mult), vb)
        wait("v", vr)
        up(V.tensor_scalar(f("sl", 1, N + 1), f("rl"), f("rl", 7, 8), None, OP.is_ge), vr)
        wait("v", vb)
        turn("ft", "fr", vb, 8)
        cast("v", 1)
        wait("v", vr)
        up(V.tensor_tensor(f("oh", 0, N), f("sl", 1, N + 1), f("sl", 0, N), OP.subtract), vc)
        wait("v", vb)
        up(V.tensor_tensor_scan(h("sa"), h("ft"), T.down[0:32, :], T.ini[0:32, 0:1], OP.add, OP.min), vb)
        up(V.tensor_tensor_scan(h("sb"), h("ft"), T.down[0:32, :], T.ini[0:32, 2:3], OP.add, OP.min), s("ac"))
        cast("v", 3)
        wait("v", vb)
        up(V.tensor_tensor_scan(h("sc", 0, NQ), h("sa"), h("sa"), -1.0, OP.max, OP.max), vb)
        wait("v", s("ac"))
        up(V.tensor_tensor_scan(h("sc", NQ, 2 * NQ), h("sb"), h("sb"), -1.0, OP.max, OP.max), vb)
        wait("v", s("nt"))
        up(V.quantize_mx(B("nq")[:, 0:130], B("nz")[:, 0:130], B("nt")[:]), s("nq"))
        wait("v", vb)
        offs, e = B("offs"), slot(core)
        for p in QUARTERS:
            up(V.tensor_scalar(offs[p:p + 32, 0:2], h("sc", NQ - 1, 2 * NQ, NQ), -1.0, NQ - 1.0, OP.mult, OP.add), s("os"))
        wait("v", vc)
        up(V.tensor_tensor(f("dd", 0, 32, 4), f("oh", 0, N), f("oh", 1, N + 1), OP.subtract), vc)
        up(V.tensor_tensor_scan(f("cb", 12, 37, 3), T.tb[:, 0:N + 1], f("sl", 1, N + 2), 0.0, OP.add, OP.mult), vr)
        wait("v", s("os"), s("nq"))
        up(V.tensor_copy(u32(s("win"), e, e + E), u32(s("nq"), 0, 130).indirect(offs[:, 0:2])), s("sl"))
        wait("s", s("nq"), s("os"))
        up(S.activation(B("wis")[:, e:e + E], B("nz")[:, 0:130].indirect(offs[:, 0:2]), AF.Copy), s("sz"))
        codes, planes = u8(s("win"), e, e + E), B("wis")[:, e:e + E]
        wait("g", s("sz"))
        send((planes, planes, aides, common, s("nb")), (planes, planes, helpers(other) + [other], local, s("nb")))
        wait("g", s("sl"))
        send((codes, codes, off, common, s("nx")), (codes, codes, [other], local, s("nx")))
        comes(s("nb"), (1 + len(same)) * wide)
        comes(s("nx"), (N - 1) * wide)
        wait("s", s("rb"))
        for c in range(8):
            up(S.activation(f("ab", EK * c + 1, EK * c + EK), ri[:, 0:RI].indirect(offs[:, 0:2]), AF.Abs,
                            bias=T.cn[:, c:c + 1], scale=1.0), s("ab"))
        wait("v", vc)
        turn("ot", "dd", vk)
        keep("v", t, t)
        keep("s", t, t)
        if t:
            keep("s", 0, 1)
        wait("v", vk)
        up(V.tensor_tensor_scan(h("ct"), h("ot"), T.zz[0:32, 0:NQ], 0.0, OP.add, OP.add), vc)
        if t:
            wait("v", "ldw")
            up(V.quantize_mx(T.wq[:], T.wz[:], T.wt[:]), "wqd")
        else:
            wait("v", "gi3")
            for i, p in enumerate(HALVES):
                up(V.tensor_scalar(T.rst[p:p + 64, 0:8 * EK:EK], T.cp[p:p + 64, 8 * i:8 * i + 8], -1.0, M + E - 1.0,
                                   OP.mult, OP.add), "rs")
        wait("v", vc, vr)
        for p in QUARTERS:
            up(V.transpose(h("cb", 0, 32, p=p), h("ct", p, p + 32)), vc)
        wait("v", vc)
        up(V.tensor_tensor_scan(f("kk", 0, 11), f("cb", 0, 44, 4), f("sl", 1, N + 4), 0.0, OP.add, OP.mult), vc)
        wait("v", s("ab"), "rs", "vz")
        up(V.tensor_tensor_scan(f("am"), f("ab"), T.rst[:], 0.0, OP.min, OP.max), vm)
        wait("v", vc)
        up(V.tensor_scalar(f("rc"), T.wp[:], f("kk", 8, 9), f("kk", 10, 11), OP.max, OP.max), vc)

        def spread(p):
            for i, q in enumerate(HALVES):
                up(V.tensor_scalar(B("offm")[p:p + 64, 8 * i:8 * i + 8], h("am", E, 8 * EK, EK, p=q, n=64), -1.0,
                                   M + E * (t + 1) - 1.0, OP.mult, OP.add), s("om"))

        if t:
            number(0, 1)
        else:
            wait("v", vm)
            spread(0)
        wait("v", vc)
        turn("lc", "rc", vc)
        wait("v", vm)
        spread(0 if t else 64)
        wait("v", vc)
        up(V.tensor_tensor_scan(h("oy"), T.old[0:32, :], h("lc"), -FAR, OP.max, OP.min), vc)
        if t:
            spread(64)
            number(1, 1)
        else:
            wait("v", s("om"), s("mc"))
            memory(0, "mp")
        wait("v", vc)
        lanes(B("offq"), "oy", float(NS), s("od"))
        if t:
            number(2, 1)
        else:
            memory(1, "m2")
        wait("s", s("om"), s("mc"))
        for i in range(2):
            up(S.activation(B("mz", t + 1)[:, H * i:H * i + H], B("mx")[:, 0:MW].indirect(B("offm")[:, 8 * i:8 * i + 8]),
                            AF.Copy), s("mo"))
        wait("s", s("od"), s("sz"), s("qc"), s("nb"))
        up(S.activation(B("qz", t + 1)[:, 0:NQ], B("wis")[:, 0:NS + NQ].indirect(B("offq")[:, 0:8]), AF.Copy), s("qp"))
        if t:
            wait("v", s("om"), s("mc"))
            memory(0, "mp")
        wait("v", s("od"), s("sl"), s("qc"), s("nx"))
        up(V.tensor_copy(u32(s("qa", t + 1), 0, NQ), u32(s("win"), 0, NS + NQ).indirect(B("offq")[:, 0:8])), s("qp"))
        if t:
            memory(1, "m2")
        else:
            again(0, 1)
            again(1, 1)

    wait("y", "wi0", "wi1")
    for u in range(R):
        up(Y.dma_start(T.wi[u:u + 1, :], T["wv%d" % u][:, 0:1]), "st", 16)
    wait("y", "mp1")
    up(Y.dma_start(T.oc[:, 0:4 * H], u8("mq%d" % R, 0, H)), "st", 16)
    wait("y", "mo1")
    for c in range(4):
        up(Y.dma_start(T.osc[4 * c:4 * c + 4, 0:M], T["mz%d" % R][32 * c:32 * c + 4, 0:M]), "st", 16)
    wait("y", "m21")
    up(Y.dma_start(T.oc[:, 4 * H:4 * M], u8("mq%d" % R, H, M)), "st", 16)
    wait("t", "wqd", "qp1")
    up(P.matmul_mx(T.pyy[:, 0:NQ], T.wq[:], T.wz[:], T.qa2[:], T.qz2[:], True, True), "yp")
    wait("v", "yp")
    up(V.tensor_copy(T.yt[:], T.pyy[:, 0:NQ]), "yc")
    wait("s", "yc")
    up(S.dma_start(T.y[:], T.yt[:]), "sty", 16)
    rest()
